import numpy as np
import ml_dtypes


def mxq(x, axis, fmt="e4m3"):
    dtype, down = {"e4m3": (ml_dtypes.float8_e4m3fn, 7), "e5m2": (ml_dtypes.float8_e5m2, 14)}[fmt]
    v = np.moveaxis(np.asarray(x, np.float32).astype(ml_dtypes.bfloat16).astype(np.float64), axis, -1)
    blocks = v.reshape(v.shape[:-1] + (-1, 32))
    amax = np.abs(blocks).max(-1, keepdims=True)
    byte = np.maximum(np.where(amax > 0, np.frexp(amax)[1] - 1 + 127, 0) - down, 1)
    scale = np.exp2(byte - 127.0)
    codes = (blocks / scale).astype(np.float32).astype(dtype).astype(np.float64)
    return np.moveaxis((codes * scale).reshape(v.shape), -1, axis)


WIDE = False


def mx_kscale(k):
    if not WIDE:
        return np.ones(k)
    levels = np.array([10, -10, 5, -5, 0])
    if k % 512:
        return np.exp2(np.random.permutation(np.resize(levels, k // 32))).repeat(32)
    a = np.empty((k // 512, 16))
    for p in range(k // 512):
        a[p, :8] = np.random.permutation(np.resize(levels, 8))
        for g in range(8):
            far = levels[np.abs(levels - a[p, g]) >= 10]
            a[p, g + 8] = far[np.random.randint(len(far))]
    return np.exp2(a.ravel()).repeat(32)


def f64(x):
    return np.asarray(x).astype(np.float64)


def striped(idx):
    return np.tile(idx.reshape(-1, 16).T, (8, 1)).astype(np.uint16)


def unstriped(offs):
    return offs[:16].T.reshape(-1).astype(np.int64)


E2M1 = np.array([0.0, 0.5, 1.0, 1.5, 2.0, 3.0, 4.0, 6.0, -0.0, -0.5, -1.0, -1.5, -2.0, -3.0, -4.0, -6.0])


def pack_weight(w, fmt):
    k, n = w.shape
    w = f64(np.asarray(w, np.float32).astype(ml_dtypes.bfloat16)).reshape(k // 32, 32, n)
    amax = np.abs(w).max(1)
    if fmt == "e4m3":
        byte = np.frexp(amax)[1] - 1 + 127 - 7
    else:
        mant, ex = np.frexp(amax / 6.0)
        byte = np.where(mant > 0.5, ex, ex - 1) + 127
    byte = np.clip(np.where(amax > 0, byte, 1), 1, 254)
    scaled = (w * np.exp2(127.0 - byte)[:, None, :]).reshape(k, n).astype(np.float32)
    by_word = np.ascontiguousarray(scaled.reshape(k // 512, 128, 4, n).transpose(0, 1, 3, 2))
    if fmt == "e4m3":
        words = by_word.astype(ml_dtypes.float8_e4m3fn).view(np.uint8)
    else:
        c = by_word.astype(ml_dtypes.float4_e2m1fn).view(np.uint8) & 0xF
        words = (c[..., 0::2] | (c[..., 1::2] << 4)).reshape(k // 512, 128, 2 * n)
    return np.ascontiguousarray(words), np.ascontiguousarray(byte.astype(np.uint8).reshape(k // 512, 16, n))


def unpack_weight(words, scales, fmt):
    g, _, n = scales.shape
    words = np.ascontiguousarray(words).reshape(g, 128, n, -1)
    if fmt == "e4m3":
        vals = words.view(ml_dtypes.float8_e4m3fn).astype(np.float64)
    else:
        nib = np.empty((g, 128, n, 4), np.uint8)
        nib[..., 0::2] = words & 0xF
        nib[..., 1::2] = words >> 4
        vals = E2M1[nib]
    vals = vals * np.repeat(np.exp2(scales.astype(np.float64) - 127.0), 8, axis=1)[..., None]
    return vals.transpose(0, 1, 3, 2).reshape(g * 512, n)


def gelu(v):
    return 0.5 * v * (1.0 + np.tanh(np.sqrt(2.0 / np.pi) * (v + 0.044715 * v**3)))


def bf(x):
    return np.asarray(x, np.float32).astype(ml_dtypes.bfloat16)


def planes(Y):
    n, m = Y.shape
    b = f64(bf(Y)).reshape(n // 32, 32, m)
    amax = np.abs(b).max(1)
    byte = np.clip(np.where(amax > 0, np.frexp(amax)[1] - 1 + 127 - 7, 1), 1, 254)
    codes = (b * np.exp2(127.0 - byte)[:, None, :]).reshape(n, m).astype(np.float32).astype(ml_dtypes.float8_e4m3fn).view(np.uint8)
    words = codes.reshape(n // 512, 128, 4, m).transpose(0, 1, 3, 2)
    return np.ascontiguousarray(words), np.ascontiguousarray(byte.astype(np.uint8).reshape(n // 512, 16, m))


K, H, N, T, S, T2 = 1024, 512, 640, 2048, 1024, 2048

def setup_inputs():
    n = np.random.standard_normal
    s = mx_kscale(K)[:, None]
    u = mx_kscale(H)[:, None]
    root = np.sqrt(u.T)
    tab_words, tab_scales = pack_weight(n((K, T)) * s, "e4m3")
    w1_words, w1_scales = pack_weight(n((K, H)) / np.sqrt(K) / s * root, "e2m1")
    w2 = (0.8 * n((K, H)) / np.sqrt(K) / s * root).astype(np.float32)
    w3_words, w3_scales = pack_weight(n((H, N)) / np.sqrt(H) / u, "e4m3")
    return {
        "tab_words": tab_words, "tab_scales": tab_scales,
        "offs": striped(np.random.permutation(T)[:S]),
        "offs2": striped(np.random.permutation(T2)[:S]),
        "w1_words": w1_words, "w1_scales": w1_scales,
        "w2": w2,
        "wgs": np.exp(0.3 * n((128, S))).astype(np.float32),
        "page0": (n((H, T2)) * u).astype(np.float32),
        "w3_words": w3_words, "w3_scales": w3_scales,
        "bias": (0.5 * n(N)).astype(np.float32),
        "site": n((N, T2)).astype(np.float32),
    }

def reference(tab_words, tab_scales, offs, offs2, w1_words, w1_scales, w2, wgs, page0, w3_words, w3_scales, bias, site):
    v = unpack_weight(tab_words, tab_scales, "e4m3")[:, unstriped(offs)]
    w1 = unpack_weight(w1_words, w1_scales, "e2m1")
    a = w1.T @ v
    b = mxq(f64(w2), 0, "e4m3").T @ v
    h = np.square(a) - np.square(b)
    page = f64(page0).copy()
    page[:, unstriped(offs2)] = np.tile(f64(wgs), (H // 128, 1)) * h
    words, scales = planes(page)
    w3 = unpack_weight(w3_words, w3_scales, "e4m3")
    e = (w3.T @ mxq(page, 0, "e4m3")) + f64(bias)[:, None]
    y = f64(site) / (1.0 + np.exp(-e))
    return y, page, words, scales

@@ -1,0 +1,300 @@
+from contextlib import ExitStack
+
+import concourse.mybir as mybir
+from concourse.masks import make_identity
+
+K, H, N, T, S = 1024, 512, 640, 2048, 1024
+FLOPS = 2 * (2 * K * H * S + H * N * T)
+
+F32 = mybir.dt.float32
+BF16 = mybir.dt.bfloat16
+I32 = mybir.dt.int32
+U32 = mybir.dt.uint32
+U16 = mybir.dt.uint16
+U8 = mybir.dt.uint8
+FP8X4 = mybir.dt.float8_e4m3fn_x4
+FP4X4 = mybir.dt.float4_e2m1fn_x4
+ACT = mybir.ActivationFunctionType
+ALU = mybir.AluOpType
+
+P = 128
+PACK = 4
+QUAD = 32
+QUADS = P // QUAD
+BANK = 512
+PASSES = K // (P * PACK)
+HALVES = S // BANK
+CHUNKS = T // BANK
+N_TILES = N // P
+LIST_COLS = BANK // 16
+TURNED = 2
+
+
+def tile_list_tumour_board_page_kernel(
+    tc, tab_words, tab_scales, offs, offs2, w1_words, w1_scales, w2, wgs, page0, w3_words, w3_scales, bias, site,
+    out_0, out_1, out_2, out_3,
+):
+    nc = tc.nc
+    with ExitStack() as ctx:
+        keep = ctx.enter_context(tc.tile_pool(name="keep", bufs=1))
+        ring = ctx.enter_context(tc.tile_pool(name="ring", bufs=4))
+        psum = ctx.enter_context(tc.psum_pool(name="psum", bufs=8))
+
+        def held(name, shape, dtype, tag=""):
+            return keep.tile(shape, dtype, name=name, tag=tag or name, align_bytes=64)
+
+        def bank(name):
+            return psum.tile([P, BANK], F32, name=name, tag="bank")
+
+        def cols(i, width=BANK):
+            return slice(i * width, (i + 1) * width)
+
+        pick = keep.tile([P, S // 16], U16, name="pick")
+        place = keep.tile([P, S // 16], U16, name="place")
+        tab_w = [held("tab_w%d" % a, [P, T], I32) for a in range(PASSES)]
+        tab_s = held("tab_s", [P, T], U8)
+        v_w = [[held("v_w0_%d" % h, [P, BANK], U32) for h in range(HALVES)], [held("v_w1_0", [P, BANK], U32)]]
+        v_s = held("v_s", [P, S], U8)
+        v_s_low = held("v_s_low", [P, S], U8)
+        w1_raw = held("w1_raw", [P, PASSES, 2 * H], U8)
+        w1_s_raw = held("w1_s_raw", [P, PASSES, H], U8)
+        w1_w = [held("w1_w%d" % a, [P, 2 * H], U8, tag="shared%d" % a) for a in range(PASSES)]
+        w1_s = held("w1_s", [P, PASSES, H], U8)
+        w2_raw = [held("w2_raw%d" % a, [P, PACK, H], F32) for a in range(PASSES)]
+        w2_bf = [held("w2_bf%d" % a, [P, PACK * H], BF16) for a in range(PASSES)]
+        w2_w = [held("w2_w%d" % a, [P, H], U32, tag="shared%d" % (PASSES + a)) for a in range(PASSES)]
+        w2_s = [held("w2_s%d" % a, [P, H], U8) for a in range(PASSES)]
+        wgs_raw = held("wgs_raw", [P, S], F32)
+        gain_late = held("gain_late", [P, PACK - TURNED, S], F32)
+        gain = [held("gain%d" % t, [P, S], F32) for t in range(TURNED)] + [gain_late[:, t, :] for t in range(PACK - TURNED)]
+        page = [held("page%d" % t, [P, T], F32) for t in range(PACK)]
+        a_sq = [held("a_sq%d" % t, [P, S], F32) for t in range(PACK)]
+        b_sq = [held("b_sq%d" % t, [P, S], F32) for t in range(PACK)]
+        w3_w = held("w3_w", [P, N], I32)
+        w3_s = held("w3_s", [P, N], U8)
+        bias_col = held("bias_col", [P, N_TILES], F32)
+        site_t = [held("site%d" % i, [P, T], F32) for i in range(N_TILES)]
+        page_w = [held("page_w%d" % g, [P, 2 * BANK], I32) for g in range(CHUNKS // 2)]
+        page_s = held("page_s", [P, T], U8)
+        ident = held("ident", [P, P], F32)
+        warm = held("warm", [P, 1], F32)
+
+        for plane in (tab_s[:], w1_s_raw[:].rearrange("p a c -> p (a c)"), v_s_low[:], w3_s[:]):
+            nc.vector.memset(plane.bitcast(I32), 0)
+        make_identity(nc, ident[:])
+        nc.scalar.activation(warm[:], ident[:, 0:1], ACT.Sigmoid)
+
+        page_rows = page0.rearrange("(p t) m -> t p m", t=PACK)
+        out_rows = out_1.rearrange("(p t) m -> t p m", t=PACK)
+
+        def load_tab(a):
+            nc.sync.dma_start(tab_w[a][:], tab_words[a].rearrange("p t i -> p (t i)").bitcast(I32))
+
+        def load_w2(a):
+            rows = w2[a * P * PACK : (a + 1) * P * PACK, :]
+            nc.sync.dma_start(w2_raw[a][:], rows.rearrange("(p j) c -> p j c", j=PACK))
+
+        nc.sync.dma_start(pick[:], offs)
+        nc.sync.dma_start(w1_raw[:].bitcast(I32), w1_words.rearrange("a p c -> p a c").bitcast(I32))
+        for q in range(QUADS):
+            nc.sync.dma_start(
+                tab_s[QUAD * q : QUAD * q + 4 * PASSES, :].bitcast(I32), tab_scales[:, 4 * q : 4 * q + 4, :].bitcast(I32)
+            )
+        nc.sync.dma_start(wgs_raw[:], wgs)
+        load_tab(0)
+        for q in range(QUADS):
+            nc.sync.dma_start(
+                w1_s_raw[QUAD * q : QUAD * q + 4, :, :].bitcast(I32),
+                w1_scales[:, 4 * q : 4 * q + 4, :].rearrange("a r c -> r a c").bitcast(I32),
+            )
+        load_tab(1)
+        for a in range(PASSES):
+            nc.vector.tensor_copy(
+                w1_w[a][:].bitcast(U16).rearrange("p (t m) -> p m t", t=PACK),
+                w1_raw[:, a, :].bitcast(U16).rearrange("p (m t) -> p m t", t=PACK),
+            )
+        nc.vector.tensor_copy(v_s[:], tab_s[:].indirect(pick[:]))
+        load_w2(0)
+        load_w2(1)
+        for q in range(QUADS):
+            nc.sync.dma_start(
+                v_s_low[QUAD * q : QUAD * q + 4, :].bitcast(I32), v_s[QUAD * q + 4 : QUAD * q + 8, :].bitcast(I32)
+            )
+        nc.sync.dma_start(place[:], offs2)
+        nc.sync.dma_start(page[0][:], page_rows[0])
+        nc.sync.dma_start(page[1][:], page_rows[1])
+        for q in (0, 2, 1, 3):
+            nc.sync.dma_start(
+                gain_late[QUAD * q : QUAD * (q + 1), :, :], wgs.rearrange("(m t) j -> m t j", t=PACK)[:, TURNED:, :]
+            )
+        nc.sync.dma_start(page[2][:], page_rows[2])
+        nc.sync.dma_start(page[3][:], page_rows[3])
+        nc.sync.dma_start(w3_w[:], w3_words[0].rearrange("p c i -> p (c i)").bitcast(I32))
+        for q in range(QUADS):
+            nc.sync.dma_start(
+                w3_s[QUAD * q : QUAD * q + 4, :].bitcast(I32), w3_scales[0, 4 * q : 4 * q + 4, :].bitcast(I32)
+            )
+        with nc.allow_non_contiguous_dma(reason="one bias value a partition"):
+            nc.sync.dma_start(bias_col[:], bias.rearrange("(i p) -> p i", p=P))
+        for i in range(N_TILES):
+            nc.sync.dma_start(site_t[i][:], site[cols(i, P), :])
+
+        turned = []
+        for h in range(HALVES):
+            first = bank("turned%d" % h)
+            for b in range(BANK // P):
+                nc.tensor.transpose(first[:, cols(b, P)], wgs_raw[:, cols(h * (BANK // P) + b, P)], ident[:])
+            turned.append(first)
+
+        def make_gain(t, h):
+            spread = ring.tile([P, BANK], F32, name="spread")
+            rows = turned[h][:].rearrange("p (b m t) -> p t b m", t=PACK, m=QUAD)[:, t]
+            nc.scalar.copy(
+                spread[:].rearrange("p (b q m) -> p b q m", q=QUADS, m=QUAD),
+                rows.unsqueeze(2).to_broadcast([P, BANK // P, QUADS, QUAD]),
+            )
+            back = bank("back")
+            for b in range(BANK // P):
+                nc.tensor.transpose(back[:, cols(b, P)], spread[:, cols(b, P)], ident[:])
+            nc.scalar.copy(gain[t][:, cols(h)], back[:])
+
+        def gather_words(a, h):
+            nc.vector.tensor_copy(v_w[a][h][:], tab_w[a][:].bitcast(U32).indirect(pick[:, cols(h, LIST_COLS)]))
+
+        def round_w2(a, split):
+            dst = w2_bf[a][:].rearrange("p (t m j) -> p m j t", t=PACK, j=PACK)
+            src = w2_raw[a][:].rearrange("p j (m t) -> p m j t", t=PACK)
+            nc.vector.tensor_copy(dst[:, :split], src[:, :split])
+            nc.scalar.copy(dst[:, split:], src[:, split:])
+
+        def quantize_w2(a, t0, t1):
+            nc.vector.quantize_mx(
+                out=w2_w[a][:, t0 * P : t1 * P].bitcast(FP8X4),
+                scales=w2_s[a][:, t0 * P : t1 * P],
+                in_=w2_bf[a][:, t0 * BANK : t1 * BANK],
+            )
+
+        for h in range(HALVES):
+            make_gain(0, h)
+        gather_words(0, 0)
+        gather_words(0, 1)
+        gather_words(1, 0)
+        nc.vector.tensor_copy(
+            w1_s[:].rearrange("p a (t m) -> p a m t", t=PACK), w1_s_raw[:].rearrange("p a (m t) -> p a m t", t=PACK)
+        )
+        round_w2(0, 88)
+        quantize_w2(0, 0, 4)
+        round_w2(1, 88)
+        quantize_w2(1, 0, 1)
+        v_w[1].append(held("v_w1_1", [P, BANK], U32, tag="w2_raw1"))
+        gather_words(1, 1)
+        quantize_w2(1, 1, 2)
+        quantize_w2(1, 2, 4)
+
+        def squares(t, h):
+            a_sum = bank("a_sum")
+            for a in reversed(range(PASSES)):
+                nc.tensor.matmul_mx(
+                    out=a_sum[:],
+                    lhsT=w1_w[a][:, cols(t, 2 * P)].bitcast(FP4X4),
+                    lhsT_scale=w1_s[:, a, cols(t, P)],
+                    rhs=v_w[a][h][:].bitcast(FP8X4),
+                    rhs_scale=(v_s, v_s_low)[a][:, cols(h)],
+                    start=(a == PASSES - 1),
+                    stop=(a == 0),
+                )
+            b_sum = bank("b_sum")
+            order = (0, 1) if t == h == 0 else (1, 0)
+            for a in order:
+                nc.tensor.matmul_mx(
+                    out=b_sum[:],
+                    lhsT=w2_w[a][:, cols(t, P)].bitcast(FP8X4),
+                    lhsT_scale=w2_s[a][:, cols(t, P)],
+                    rhs=v_w[a][h][:].bitcast(FP8X4),
+                    rhs_scale=v_s[4 * a :, cols(h)],
+                    start=(a == order[0]),
+                    stop=(a == order[-1]),
+                )
+            nc.scalar.activation(a_sq[t][:, cols(h)], a_sum[:], ACT.Square)
+            nc.scalar.activation(b_sq[t][:, cols(h)], b_sum[:], ACT.Square)
+
+        def scatter(t, lo, hi):
+            nc.vector.tensor_tensor(a_sq[t][:, lo:hi], a_sq[t][:, lo:hi], b_sq[t][:, lo:hi], ALU.subtract)
+            nc.vector.tensor_tensor(
+                page[t][:].indirect(place[:, lo // 16 : hi // 16]), a_sq[t][:, lo:hi], gain[t][:, lo:hi], ALU.mult
+            )
+
+        for t in range(PACK):
+            for h in range(HALVES):
+                if 0 < t < TURNED:
+                    make_gain(t, h)
+                squares(t, h)
+                if t == 0:
+                    scatter(t, h * BANK, (h + 1) * BANK)
+            if t > 0:
+                scatter(t, 0, S)
+
+        page_bf = [held("page_bf%d" % c, [P, BANK, PACK], BF16, tag="shared%d" % c) for c in range(CHUNKS)]
+        for t in range(PACK):
+            nc.sync.dma_start(out_rows[t], page[t][:])
+            if t < PACK - 2:
+                for c in range(CHUNKS):
+                    nc.scalar.copy(page_bf[c][:, :, t], page[t][:, cols(c)])
+            if t == PACK - 2:
+                for c in range(CHUNKS):
+                    nc.scalar.copy(page_bf[c][:, :, t:], page[t][:, cols(c)].unsqueeze(2).to_broadcast([P, BANK, 2]))
+
+        codes_out = out_2[0].rearrange("p m i -> p (m i)").bitcast(I32)
+
+        def last_plane(copy, c, lo, hi):
+            copy(page_bf[c][:, lo:hi, PACK - 1], page[PACK - 1][:, c * BANK + lo : c * BANK + hi])
+
+        def quantize_page(c):
+            nc.vector.quantize_mx(
+                out=page_w[c // 2][:, cols(c % 2)].bitcast(FP8X4),
+                scales=page_s[:, cols(c)],
+                in_=page_bf[c][:].rearrange("p m t -> p (m t)"),
+            )
+            if c % 2 == 1:
+                nc.sync.dma_start(codes_out[:, cols(c // 2, 2 * BANK)], page_w[c // 2][:])
+
+        def gate(g, i, pieces):
+            sig = ring.tile([P, 2 * BANK], F32, name="sig", bufs=3)
+            for u in range(2):
+                e_sum = bank("e_sum")
+                nc.tensor.matmul_mx(
+                    out=e_sum[:],
+                    lhsT=w3_w[:, cols(i, P)].bitcast(FP8X4),
+                    lhsT_scale=w3_s[:, cols(i, P)],
+                    rhs=page_w[g][:, cols(u)].bitcast(FP8X4),
+                    rhs_scale=page_s[:, cols(2 * g + u)],
+                    start=True,
+                    stop=True,
+                )
+                nc.scalar.activation(sig[:, cols(u)], e_sum[:], ACT.Sigmoid, bias=bias_col[:, i : i + 1])
+            width = 2 * BANK // pieces
+            for u in range(pieces):
+                m_cols = cols(g * pieces + u, width)
+                nc.vector.tensor_tensor(site_t[i][:, m_cols], sig[:, cols(u, width)], site_t[i][:, m_cols], ALU.mult)
+                nc.sync.dma_start(out_0[cols(i, P), m_cols], site_t[i][:, m_cols])
+
+        last_plane(nc.vector.tensor_copy, 0, 0, BANK)
+        last_plane(nc.scalar.copy, 1, 0, BANK)
+        last_plane(nc.scalar.copy, 3, 0, BANK // 2)
+        quantize_page(0)
+        last_plane(nc.vector.tensor_copy, 2, 0, BANK)
+        quantize_page(1)
+        gate(0, 0, 1)
+        quantize_page(2)
+        gate(0, 1, 1)
+        last_plane(nc.vector.tensor_copy, 3, BANK // 2, BANK)
+        gate(0, 2, 1)
+        quantize_page(3)
+        for q in range(QUADS):
+            nc.sync.dma_start(
+                out_3[0, 4 * q : 4 * q + 4, :].bitcast(I32), page_s[QUAD * q : QUAD * q + 4, :].bitcast(I32)
+            )
+        gate(0, 3, 1)
+        gate(0, 4, 1)
+        for i in range(N_TILES):
+            gate(1, i, 2 if i == N_TILES - 1 else 1)

@@ -53,7 +53,7 @@ def tile_list_tumour_board_page_kernel(
         place = keep.tile([P, S // 16], U16, name="place")
         tab_w = [held("tab_w%d" % a, [P, T], I32) for a in range(PASSES)]
         tab_s = held("tab_s", [P, T], U8)
-        v_w = [[held("v_w0_%d" % h, [P, BANK], U32) for h in range(HALVES)], [held("v_w1_0", [P, BANK], U32)]]
+        v_w = [[held("v_w%d_%d" % (a, h), [P, BANK], U32) for h in range(HALVES)] for a in range(PASSES)]
         v_s = held("v_s", [P, S], U8)
         v_s_low = held("v_s_low", [P, S], U8)
         w1_raw = held("w1_raw", [P, PASSES, 2 * H], U8)
@@ -114,12 +114,12 @@ def tile_list_tumour_board_page_kernel(
                 w1_raw[:, a, :].bitcast(U16).rearrange("p (m t) -> p m t", t=PACK),
             )
         nc.vector.tensor_copy(v_s[:], tab_s[:].indirect(pick[:]))
-        load_w2(0)
-        load_w2(1)
         for q in range(QUADS):
             nc.sync.dma_start(
                 v_s_low[QUAD * q : QUAD * q + 4, :].bitcast(I32), v_s[QUAD * q + 4 : QUAD * q + 8, :].bitcast(I32)
             )
+        load_w2(0)
+        load_w2(1)
         nc.sync.dma_start(place[:], offs2)
         nc.sync.dma_start(page[0][:], page_rows[0])
         nc.sync.dma_start(page[1][:], page_rows[1])
@@ -161,11 +161,10 @@ def tile_list_tumour_board_page_kernel(
         def gather_words(a, h):
             nc.vector.tensor_copy(v_w[a][h][:], tab_w[a][:].bitcast(U32).indirect(pick[:, cols(h, LIST_COLS)]))
 
-        def round_w2(a, split):
+        def round_w2(copy, a, lo, hi):
             dst = w2_bf[a][:].rearrange("p (t m j) -> p m j t", t=PACK, j=PACK)
             src = w2_raw[a][:].rearrange("p j (m t) -> p m j t", t=PACK)
-            nc.vector.tensor_copy(dst[:, :split], src[:, :split])
-            nc.scalar.copy(dst[:, split:], src[:, split:])
+            copy(dst[:, lo:hi], src[:, lo:hi])
 
         def quantize_w2(a, t0, t1):
             nc.vector.quantize_mx(
@@ -174,24 +173,24 @@ def tile_list_tumour_board_page_kernel(
                 in_=w2_bf[a][:, t0 * BANK : t1 * BANK],
             )
 
-        for h in range(HALVES):
-            make_gain(0, h)
-        gather_words(0, 0)
-        gather_words(0, 1)
-        gather_words(1, 0)
+        for t in range(TURNED):
+            for h in range(HALVES):
+                make_gain(t, h)
+        for a in range(PASSES):
+            for h in range(HALVES):
+                gather_words(a, h)
         nc.vector.tensor_copy(
             w1_s[:].rearrange("p a (t m) -> p a m t", t=PACK), w1_s_raw[:].rearrange("p a (m t) -> p a m t", t=PACK)
         )
-        round_w2(0, 88)
+        round_w2(nc.vector.tensor_copy, 0, 0, P)
         quantize_w2(0, 0, 4)
-        round_w2(1, 88)
+        round_w2(nc.vector.tensor_copy, 1, 0, 104)
+        round_w2(nc.scalar.copy, 1, 104, P)
         quantize_w2(1, 0, 1)
-        v_w[1].append(held("v_w1_1", [P, BANK], U32, tag="w2_raw1"))
-        gather_words(1, 1)
         quantize_w2(1, 1, 2)
         quantize_w2(1, 2, 4)
 
-        def squares(t, h):
+        def square_a(t, h):
             a_sum = bank("a_sum")
             for a in reversed(range(PASSES)):
                 nc.tensor.matmul_mx(
@@ -203,6 +202,9 @@ def tile_list_tumour_board_page_kernel(
                     start=(a == PASSES - 1),
                     stop=(a == 0),
                 )
+            nc.scalar.activation(a_sq[t][:, cols(h)], a_sum[:], ACT.Square)
+
+        def square_b(t, h):
             b_sum = bank("b_sum")
             order = (0, 1) if t == h == 0 else (1, 0)
             for a in order:
@@ -215,23 +217,28 @@ def tile_list_tumour_board_page_kernel(
                     start=(a == order[0]),
                     stop=(a == order[-1]),
                 )
-            nc.scalar.activation(a_sq[t][:, cols(h)], a_sum[:], ACT.Square)
             nc.scalar.activation(b_sq[t][:, cols(h)], b_sum[:], ACT.Square)
 
-        def scatter(t, lo, hi):
-            nc.vector.tensor_tensor(a_sq[t][:, lo:hi], a_sq[t][:, lo:hi], b_sq[t][:, lo:hi], ALU.subtract)
-            nc.vector.tensor_tensor(
-                page[t][:].indirect(place[:, lo // 16 : hi // 16]), a_sq[t][:, lo:hi], gain[t][:, lo:hi], ALU.mult
-            )
+        def weigh(engine, t, h):
+            diff = held("diff_first" if t == h == 0 else "diff", [P, BANK], F32)
+            engine.tensor_tensor(diff[:], a_sq[t][:, cols(h)], b_sq[t][:, cols(h)], ALU.subtract)
+            engine.tensor_tensor(a_sq[t][:, cols(h)], diff[:], gain[t][:, cols(h)], ALU.mult)
 
+        def scatter(t, lo, hi):
+            nc.vector.tensor_copy(page[t][:].indirect(place[:, lo // 16 : hi // 16]), a_sq[t][:, lo:hi])
+
+        for t in range(2):
+            for h in range(HALVES):
+                square_a(t, h)
         for t in range(PACK):
             for h in range(HALVES):
-                if 0 < t < TURNED:
-                    make_gain(t, h)
-                squares(t, h)
-                if t == 0:
+                if t >= 2:
+                    square_a(t, h)
+                square_b(t, h)
+                weigh(nc.vector if t == h == 0 else nc.gpsimd, t, h)
+                if t < 2:
                     scatter(t, h * BANK, (h + 1) * BANK)
-            if t > 0:
+            if t >= 2:
                 scatter(t, 0, S)
 
         page_bf = [held("page_bf%d" % c, [P, BANK, PACK], BF16, tag="shared%d" % c) for c in range(CHUNKS)]
@@ -246,8 +253,8 @@ def tile_list_tumour_board_page_kernel(
 
         codes_out = out_2[0].rearrange("p m i -> p (m i)").bitcast(I32)
 
-        def last_plane(copy, c, lo, hi):
-            copy(page_bf[c][:, lo:hi, PACK - 1], page[PACK - 1][:, c * BANK + lo : c * BANK + hi])
+        def last_plane(copy, c):
+            copy(page_bf[c][:, :, PACK - 1], page[PACK - 1][:, cols(c)])
 
         def quantize_page(c):
             nc.vector.quantize_mx(
@@ -255,10 +262,10 @@ def tile_list_tumour_board_page_kernel(
                 scales=page_s[:, cols(c)],
                 in_=page_bf[c][:].rearrange("p m t -> p (m t)"),
             )
-            if c % 2 == 1:
+            if c in (1, 2):
                 nc.sync.dma_start(codes_out[:, cols(c // 2, 2 * BANK)], page_w[c // 2][:])
 
-        def gate(g, i, pieces):
+        def gate(g, i, widths):
             sig = ring.tile([P, 2 * BANK], F32, name="sig", bufs=3)
             for u in range(2):
                 e_sum = bank("e_sum")
@@ -272,29 +279,26 @@ def tile_list_tumour_board_page_kernel(
                     stop=True,
                 )
                 nc.scalar.activation(sig[:, cols(u)], e_sum[:], ACT.Sigmoid, bias=bias_col[:, i : i + 1])
-            width = 2 * BANK // pieces
-            for u in range(pieces):
-                m_cols = cols(g * pieces + u, width)
-                nc.vector.tensor_tensor(site_t[i][:, m_cols], sig[:, cols(u, width)], site_t[i][:, m_cols], ALU.mult)
+            lo = 0
+            for width in widths:
+                m_cols = slice(2 * BANK * g + lo, 2 * BANK * g + lo + width)
+                nc.vector.tensor_tensor(site_t[i][:, m_cols], sig[:, lo : lo + width], site_t[i][:, m_cols], ALU.mult)
                 nc.sync.dma_start(out_0[cols(i, P), m_cols], site_t[i][:, m_cols])
+                lo = lo + width
 
-        last_plane(nc.vector.tensor_copy, 0, 0, BANK)
-        last_plane(nc.scalar.copy, 1, 0, BANK)
-        last_plane(nc.scalar.copy, 3, 0, BANK // 2)
+        last_plane(nc.vector.tensor_copy, 0)
+        last_plane(nc.scalar.copy, 1)
+        last_plane(nc.scalar.copy, 3)
         quantize_page(0)
-        last_plane(nc.vector.tensor_copy, 2, 0, BANK)
         quantize_page(1)
-        gate(0, 0, 1)
-        quantize_page(2)
-        gate(0, 1, 1)
-        last_plane(nc.vector.tensor_copy, 3, BANK // 2, BANK)
-        gate(0, 2, 1)
+        last_plane(nc.vector.tensor_copy, 2)
         quantize_page(3)
-        for q in range(QUADS):
-            nc.sync.dma_start(
-                out_3[0, 4 * q : 4 * q + 4, :].bitcast(I32), page_s[QUAD * q : QUAD * q + 4, :].bitcast(I32)
-            )
-        gate(0, 3, 1)
-        gate(0, 4, 1)
-        for i in range(N_TILES):
-            gate(1, i, 2 if i == N_TILES - 1 else 1)
+        quantize_page(2)
+        for g in range(CHUNKS // 2):
+            for i in range(N_TILES):
+                gate(g, i, (512, 256, 256) if (g, i) == (CHUNKS // 2 - 1, N_TILES - 1) else (1024,))
+            if g == 0:
+                for q in range(QUADS):
+                    nc.sync.dma_start(
+                        out_3[0, 4 * q : 4 * q + 4, :].bitcast(I32), page_s[QUAD * q : QUAD * q + 4, :].bitcast(I32)
+                    )

@@ -21,13 +21,18 @@ P = 128
 PACK = 4
 QUAD = 32
 QUADS = P // QUAD
+SCALE_ROWS = 4
 BANK = 512
 PASSES = K // (P * PACK)
 HALVES = S // BANK
-CHUNKS = T // BANK
-N_TILES = N // P
 LIST_COLS = BANK // 16
+CHUNKS = T // BANK
+PAIR = 2 * BANK
+N_TILES = N // P
 TURNED = 2
+ROUND_SPLIT = 104
+EARLY = 2
+LAST_WIDTHS = (512, 256, 256)
 
 
 def tile_list_tumour_board_page_kernel(
@@ -46,8 +51,11 @@ def tile_list_tumour_board_page_kernel(
         def bank(name):
             return psum.tile([P, BANK], F32, name=name, tag="bank")
 
-        def cols(i, width=BANK):
-            return slice(i * width, (i + 1) * width)
+        def cols(index, width=BANK):
+            return slice(index * width, (index + 1) * width)
+
+        def rows_of(quad, count, first=0):
+            return slice(QUAD * quad + first, QUAD * quad + first + count)
 
         pick = keep.tile([P, S // 16], U16, name="pick")
         place = keep.tile([P, S // 16], U16, name="place")
@@ -66,7 +74,8 @@ def tile_list_tumour_board_page_kernel(
         w2_s = [held("w2_s%d" % a, [P, H], U8) for a in range(PASSES)]
         wgs_raw = held("wgs_raw", [P, S], F32)
         gain_late = held("gain_late", [P, PACK - TURNED, S], F32)
-        gain = [held("gain%d" % t, [P, S], F32) for t in range(TURNED)] + [gain_late[:, t, :] for t in range(PACK - TURNED)]
+        gain = [held("gain%d" % t, [P, S], F32) for t in range(TURNED)]
+        gain = gain + [gain_late[:, t, :] for t in range(PACK - TURNED)]
         page = [held("page%d" % t, [P, T], F32) for t in range(PACK)]
         a_sq = [held("a_sq%d" % t, [P, S], F32) for t in range(PACK)]
         b_sq = [held("b_sq%d" % t, [P, S], F32) for t in range(PACK)]
@@ -74,15 +83,13 @@ def tile_list_tumour_board_page_kernel(
         w3_s = held("w3_s", [P, N], U8)
         bias_col = held("bias_col", [P, N_TILES], F32)
         site_t = [held("site%d" % i, [P, T], F32) for i in range(N_TILES)]
-        page_w = [held("page_w%d" % g, [P, 2 * BANK], I32) for g in range(CHUNKS // 2)]
+        page_w = [held("page_w%d" % g, [P, PAIR], I32) for g in range(CHUNKS // 2)]
         page_s = held("page_s", [P, T], U8)
         ident = held("ident", [P, P], F32)
-        warm = held("warm", [P, 1], F32)
 
-        for plane in (tab_s[:], w1_s_raw[:].rearrange("p a c -> p (a c)"), v_s_low[:], w3_s[:]):
-            nc.vector.memset(plane.bitcast(I32), 0)
+        for scale_tile in (tab_s[:], w1_s_raw[:].rearrange("p a c -> p (a c)"), v_s_low[:], w3_s[:]):
+            nc.vector.memset(scale_tile.bitcast(I32), 0)
         make_identity(nc, ident[:])
-        nc.scalar.activation(warm[:], ident[:, 0:1], ACT.Sigmoid)
 
         page_rows = page0.rearrange("(p t) m -> t p m", t=PACK)
         out_rows = out_1.rearrange("(p t) m -> t p m", t=PACK)
@@ -91,23 +98,25 @@ def tile_list_tumour_board_page_kernel(
             nc.sync.dma_start(tab_w[a][:], tab_words[a].rearrange("p t i -> p (t i)").bitcast(I32))
 
         def load_w2(a):
-            rows = w2[a * P * PACK : (a + 1) * P * PACK, :]
-            nc.sync.dma_start(w2_raw[a][:], rows.rearrange("(p j) c -> p j c", j=PACK))
+            k_rows = w2[cols(a, P * PACK), :]
+            nc.sync.dma_start(w2_raw[a][:], k_rows.rearrange("(p j) c -> p j c", j=PACK))
 
         nc.sync.dma_start(pick[:], offs)
         nc.sync.dma_start(w1_raw[:].bitcast(I32), w1_words.rearrange("a p c -> p a c").bitcast(I32))
         for q in range(QUADS):
             nc.sync.dma_start(
-                tab_s[QUAD * q : QUAD * q + 4 * PASSES, :].bitcast(I32), tab_scales[:, 4 * q : 4 * q + 4, :].bitcast(I32)
+                tab_s[rows_of(q, SCALE_ROWS * PASSES), :].bitcast(I32),
+                tab_scales[:, cols(q, SCALE_ROWS), :].bitcast(I32),
             )
         nc.sync.dma_start(wgs_raw[:], wgs)
         load_tab(0)
         for q in range(QUADS):
             nc.sync.dma_start(
-                w1_s_raw[QUAD * q : QUAD * q + 4, :, :].bitcast(I32),
-                w1_scales[:, 4 * q : 4 * q + 4, :].rearrange("a r c -> r a c").bitcast(I32),
+                w1_s_raw[rows_of(q, SCALE_ROWS), :, :].bitcast(I32),
+                w1_scales[:, cols(q, SCALE_ROWS), :].rearrange("a r c -> r a c").bitcast(I32),
             )
         load_tab(1)
+
         for a in range(PASSES):
             nc.vector.tensor_copy(
                 w1_w[a][:].bitcast(U16).rearrange("p (t m) -> p m t", t=PACK),
@@ -116,8 +125,10 @@ def tile_list_tumour_board_page_kernel(
         nc.vector.tensor_copy(v_s[:], tab_s[:].indirect(pick[:]))
         for q in range(QUADS):
             nc.sync.dma_start(
-                v_s_low[QUAD * q : QUAD * q + 4, :].bitcast(I32), v_s[QUAD * q + 4 : QUAD * q + 8, :].bitcast(I32)
+                v_s_low[rows_of(q, SCALE_ROWS), :].bitcast(I32),
+                v_s[rows_of(q, SCALE_ROWS, first=SCALE_ROWS), :].bitcast(I32),
             )
+
         load_w2(0)
         load_w2(1)
         nc.sync.dma_start(place[:], offs2)
@@ -125,14 +136,14 @@ def tile_list_tumour_board_page_kernel(
         nc.sync.dma_start(page[1][:], page_rows[1])
         for q in (0, 2, 1, 3):
             nc.sync.dma_start(
-                gain_late[QUAD * q : QUAD * (q + 1), :, :], wgs.rearrange("(m t) j -> m t j", t=PACK)[:, TURNED:, :]
+                gain_late[rows_of(q, QUAD), :, :], wgs.rearrange("(m t) j -> m t j", t=PACK)[:, TURNED:, :]
             )
         nc.sync.dma_start(page[2][:], page_rows[2])
         nc.sync.dma_start(page[3][:], page_rows[3])
         nc.sync.dma_start(w3_w[:], w3_words[0].rearrange("p c i -> p (c i)").bitcast(I32))
         for q in range(QUADS):
             nc.sync.dma_start(
-                w3_s[QUAD * q : QUAD * q + 4, :].bitcast(I32), w3_scales[0, 4 * q : 4 * q + 4, :].bitcast(I32)
+                w3_s[rows_of(q, SCALE_ROWS), :].bitcast(I32), w3_scales[0, cols(q, SCALE_ROWS), :].bitcast(I32)
             )
         with nc.allow_non_contiguous_dma(reason="one bias value a partition"):
             nc.sync.dma_start(bias_col[:], bias.rearrange("(i p) -> p i", p=P))
@@ -148,10 +159,10 @@ def tile_list_tumour_board_page_kernel(
 
         def make_gain(t, h):
             spread = ring.tile([P, BANK], F32, name="spread")
-            rows = turned[h][:].rearrange("p (b m t) -> p t b m", t=PACK, m=QUAD)[:, t]
+            picked = turned[h][:].rearrange("p (b m t) -> p t b m", t=PACK, m=QUAD)[:, t]
             nc.scalar.copy(
                 spread[:].rearrange("p (b q m) -> p b q m", q=QUADS, m=QUAD),
-                rows.unsqueeze(2).to_broadcast([P, BANK // P, QUADS, QUAD]),
+                picked.unsqueeze(2).to_broadcast([P, BANK // P, QUADS, QUAD]),
             )
             back = bank("back")
             for b in range(BANK // P):
@@ -179,16 +190,16 @@ def tile_list_tumour_board_page_kernel(
         for a in range(PASSES):
             for h in range(HALVES):
                 gather_words(a, h)
-        nc.vector.tensor_copy(
-            w1_s[:].rearrange("p a (t m) -> p a m t", t=PACK), w1_s_raw[:].rearrange("p a (m t) -> p a m t", t=PACK)
+        nc.gpsimd.tensor_copy(
+            w1_s[:].rearrange("p a (t m) -> p a t m", t=PACK), w1_s_raw[:].rearrange("p a (m t) -> p a t m", t=PACK)
         )
         round_w2(nc.vector.tensor_copy, 0, 0, P)
-        quantize_w2(0, 0, 4)
-        round_w2(nc.vector.tensor_copy, 1, 0, 104)
-        round_w2(nc.scalar.copy, 1, 104, P)
+        quantize_w2(0, 0, PACK)
+        round_w2(nc.vector.tensor_copy, 1, 0, ROUND_SPLIT)
+        round_w2(nc.scalar.copy, 1, ROUND_SPLIT, P)
         quantize_w2(1, 0, 1)
         quantize_w2(1, 1, 2)
-        quantize_w2(1, 2, 4)
+        quantize_w2(1, 2, PACK)
 
         def square_a(t, h):
             a_sum = bank("a_sum")
@@ -213,33 +224,30 @@ def tile_list_tumour_board_page_kernel(
                     lhsT=w2_w[a][:, cols(t, P)].bitcast(FP8X4),
                     lhsT_scale=w2_s[a][:, cols(t, P)],
                     rhs=v_w[a][h][:].bitcast(FP8X4),
-                    rhs_scale=v_s[4 * a :, cols(h)],
+                    rhs_scale=v_s[SCALE_ROWS * a :, cols(h)],
                     start=(a == order[0]),
                     stop=(a == order[-1]),
                 )
             nc.scalar.activation(b_sq[t][:, cols(h)], b_sum[:], ACT.Square)
 
-        def weigh(engine, t, h):
-            diff = held("diff_first" if t == h == 0 else "diff", [P, BANK], F32)
+        def weigh(engine, buffer, t, h):
+            diff = held(buffer, [P, BANK], F32)
             engine.tensor_tensor(diff[:], a_sq[t][:, cols(h)], b_sq[t][:, cols(h)], ALU.subtract)
             engine.tensor_tensor(a_sq[t][:, cols(h)], diff[:], gain[t][:, cols(h)], ALU.mult)
 
-        def scatter(t, lo, hi):
-            nc.vector.tensor_copy(page[t][:].indirect(place[:, lo // 16 : hi // 16]), a_sq[t][:, lo:hi])
-
-        for t in range(2):
+        for t in range(EARLY):
             for h in range(HALVES):
                 square_a(t, h)
         for t in range(PACK):
             for h in range(HALVES):
-                if t >= 2:
+                if t >= EARLY:
                     square_a(t, h)
                 square_b(t, h)
-                weigh(nc.vector if t == h == 0 else nc.gpsimd, t, h)
-                if t < 2:
-                    scatter(t, h * BANK, (h + 1) * BANK)
-            if t >= 2:
-                scatter(t, 0, S)
+                if t == h == 0:
+                    weigh(nc.vector, "diff_first", t, h)
+                else:
+                    weigh(nc.gpsimd, "diff", t, h)
+                nc.vector.tensor_copy(page[t][:].indirect(place[:, cols(h, LIST_COLS)]), a_sq[t][:, cols(h)])
 
         page_bf = [held("page_bf%d" % c, [P, BANK, PACK], BF16, tag="shared%d" % c) for c in range(CHUNKS)]
         for t in range(PACK):
@@ -249,11 +257,15 @@ def tile_list_tumour_board_page_kernel(
                     nc.scalar.copy(page_bf[c][:, :, t], page[t][:, cols(c)])
             if t == PACK - 2:
                 for c in range(CHUNKS):
-                    nc.scalar.copy(page_bf[c][:, :, t:], page[t][:, cols(c)].unsqueeze(2).to_broadcast([P, BANK, 2]))
+                    twice = page[t][:, cols(c)].unsqueeze(2).to_broadcast([P, BANK, 2])
+                    if c < CHUNKS // 2:
+                        nc.scalar.copy(page_bf[c][:, :, t:], twice)
+                    else:
+                        nc.gpsimd.tensor_scalar(page_bf[c][:, :, t:], twice, 1.0, 0.0, ALU.mult, ALU.add)
 
         codes_out = out_2[0].rearrange("p m i -> p (m i)").bitcast(I32)
 
-        def last_plane(copy, c):
+        def round_last_slice(copy, c):
             copy(page_bf[c][:, :, PACK - 1], page[PACK - 1][:, cols(c)])
 
         def quantize_page(c):
@@ -262,11 +274,12 @@ def tile_list_tumour_board_page_kernel(
                 scales=page_s[:, cols(c)],
                 in_=page_bf[c][:].rearrange("p m t -> p (m t)"),
             )
-            if c in (1, 2):
-                nc.sync.dma_start(codes_out[:, cols(c // 2, 2 * BANK)], page_w[c // 2][:])
+
+        def store_codes(g):
+            nc.sync.dma_start(codes_out[:, cols(g, PAIR)], page_w[g][:])
 
         def gate(g, i, widths):
-            sig = ring.tile([P, 2 * BANK], F32, name="sig", bufs=3)
+            sig = ring.tile([P, PAIR], F32, name="sig", bufs=3)
             for u in range(2):
                 e_sum = bank("e_sum")
                 nc.tensor.matmul_mx(
@@ -281,24 +294,26 @@ def tile_list_tumour_board_page_kernel(
                 nc.scalar.activation(sig[:, cols(u)], e_sum[:], ACT.Sigmoid, bias=bias_col[:, i : i + 1])
             lo = 0
             for width in widths:
-                m_cols = slice(2 * BANK * g + lo, 2 * BANK * g + lo + width)
+                m_cols = slice(PAIR * g + lo, PAIR * g + lo + width)
                 nc.vector.tensor_tensor(site_t[i][:, m_cols], sig[:, lo : lo + width], site_t[i][:, m_cols], ALU.mult)
                 nc.sync.dma_start(out_0[cols(i, P), m_cols], site_t[i][:, m_cols])
                 lo = lo + width
 
-        last_plane(nc.vector.tensor_copy, 0)
-        last_plane(nc.scalar.copy, 1)
-        last_plane(nc.scalar.copy, 3)
+        round_last_slice(nc.vector.tensor_copy, 0)
+        round_last_slice(nc.scalar.copy, 1)
         quantize_page(0)
         quantize_page(1)
-        last_plane(nc.vector.tensor_copy, 2)
-        quantize_page(3)
+        store_codes(0)
+        round_last_slice(nc.vector.tensor_copy, 2)
+        round_last_slice(nc.vector.tensor_copy, 3)
         quantize_page(2)
-        for g in range(CHUNKS // 2):
-            for i in range(N_TILES):
-                gate(g, i, (512, 256, 256) if (g, i) == (CHUNKS // 2 - 1, N_TILES - 1) else (1024,))
-            if g == 0:
-                for q in range(QUADS):
-                    nc.sync.dma_start(
-                        out_3[0, 4 * q : 4 * q + 4, :].bitcast(I32), page_s[QUAD * q : QUAD * q + 4, :].bitcast(I32)
-                    )
+        quantize_page(3)
+        store_codes(1)
+        for i in range(N_TILES):
+            gate(0, i, (PAIR,))
+        for q in range(QUADS):
+            nc.sync.dma_start(
+                out_3[0, cols(q, SCALE_ROWS), :].bitcast(I32), page_s[rows_of(q, SCALE_ROWS), :].bitcast(I32)
+            )
+        for i in range(N_TILES):
+            gate(1, i, LAST_WIDTHS if i == N_TILES - 1 else (PAIR,))

@@ -30,9 +30,13 @@ CHUNKS = T // BANK
 PAIR = 2 * BANK
 N_TILES = N // P
 TURNED = 2
-ROUND_SPLIT = 104
-EARLY = 2
+EARLY = 1
+SITE_FIRST = 3
+FIRST_BANKS = (7, 1)
+A_BANKS = ((6, 0), (7, 1), (3, 4), (5, 6))
+B_BANKS = ((None, 3), (4, 5), (6, 0), (7, 1))
 LAST_WIDTHS = (512, 256, 256)
+PAIRED = 2 * N_TILES - 2
 
 
 def tile_list_tumour_board_page_kernel(
@@ -43,13 +47,13 @@ def tile_list_tumour_board_page_kernel(
     with ExitStack() as ctx:
         keep = ctx.enter_context(tc.tile_pool(name="keep", bufs=1))
         ring = ctx.enter_context(tc.tile_pool(name="ring", bufs=4))
-        psum = ctx.enter_context(tc.psum_pool(name="psum", bufs=8))
+        psum = ctx.enter_context(tc.psum_pool(name="psum", bufs=1))
 
         def held(name, shape, dtype, tag=""):
             return keep.tile(shape, dtype, name=name, tag=tag or name, align_bytes=64)
 
-        def bank(name):
-            return psum.tile([P, BANK], F32, name=name, tag="bank")
+        def bank(name, number):
+            return psum.tile([P, BANK], F32, name=name, tag="bank%d" % number)
 
         def cols(index, width=BANK):
             return slice(index * width, (index + 1) * width)
@@ -90,6 +94,8 @@ def tile_list_tumour_board_page_kernel(
         for scale_tile in (tab_s[:], w1_s_raw[:].rearrange("p a c -> p (a c)"), v_s_low[:], w3_s[:]):
             nc.vector.memset(scale_tile.bitcast(I32), 0)
         make_identity(nc, ident[:])
+        warm = held("warm", [P, 1], F32)
+        nc.scalar.activation(warm[:], ident[:, 0:1], ACT.Sigmoid)
 
         page_rows = page0.rearrange("(p t) m -> t p m", t=PACK)
         out_rows = out_1.rearrange("(p t) m -> t p m", t=PACK)
@@ -115,6 +121,7 @@ def tile_list_tumour_board_page_kernel(
                 w1_s_raw[rows_of(q, SCALE_ROWS), :, :].bitcast(I32),
                 w1_scales[:, cols(q, SCALE_ROWS), :].rearrange("a r c -> r a c").bitcast(I32),
             )
+        load_w2(0)
         load_tab(1)
 
         for a in range(PASSES):
@@ -129,7 +136,6 @@ def tile_list_tumour_board_page_kernel(
                 v_s[rows_of(q, SCALE_ROWS, first=SCALE_ROWS), :].bitcast(I32),
             )
 
-        load_w2(0)
         load_w2(1)
         nc.sync.dma_start(place[:], offs2)
         nc.sync.dma_start(page[0][:], page_rows[0])
@@ -139,7 +145,6 @@ def tile_list_tumour_board_page_kernel(
                 gain_late[rows_of(q, QUAD), :, :], wgs.rearrange("(m t) j -> m t j", t=PACK)[:, TURNED:, :]
             )
         nc.sync.dma_start(page[2][:], page_rows[2])
-        nc.sync.dma_start(page[3][:], page_rows[3])
         nc.sync.dma_start(w3_w[:], w3_words[0].rearrange("p c i -> p (c i)").bitcast(I32))
         for q in range(QUADS):
             nc.sync.dma_start(
@@ -148,11 +153,14 @@ def tile_list_tumour_board_page_kernel(
         with nc.allow_non_contiguous_dma(reason="one bias value a partition"):
             nc.sync.dma_start(bias_col[:], bias.rearrange("(i p) -> p i", p=P))
         for i in range(N_TILES):
+            if i == SITE_FIRST:
+                nc.sync.dma_start(page[3][:], page_rows[3])
             nc.sync.dma_start(site_t[i][:], site[cols(i, P), :])
 
+        gain_first = bank("gain_first", 2)
         turned = []
         for h in range(HALVES):
-            first = bank("turned%d" % h)
+            first = bank("turned%d" % h, h)
             for b in range(BANK // P):
                 nc.tensor.transpose(first[:, cols(b, P)], wgs_raw[:, cols(h * (BANK // P) + b, P)], ident[:])
             turned.append(first)
@@ -164,18 +172,19 @@ def tile_list_tumour_board_page_kernel(
                 spread[:].rearrange("p (b q m) -> p b q m", q=QUADS, m=QUAD),
                 picked.unsqueeze(2).to_broadcast([P, BANK // P, QUADS, QUAD]),
             )
-            back = bank("back")
+            back = gain_first if t == h == 0 else bank("back", 2 + HALVES * t + h)
             for b in range(BANK // P):
                 nc.tensor.transpose(back[:, cols(b, P)], spread[:, cols(b, P)], ident[:])
-            nc.scalar.copy(gain[t][:, cols(h)], back[:])
+            if back is not gain_first:
+                nc.scalar.copy(gain[t][:, cols(h)], back[:])
 
         def gather_words(a, h):
             nc.vector.tensor_copy(v_w[a][h][:], tab_w[a][:].bitcast(U32).indirect(pick[:, cols(h, LIST_COLS)]))
 
-        def round_w2(copy, a, lo, hi):
+        def round_w2(a, t0, t1):
             dst = w2_bf[a][:].rearrange("p (t m j) -> p m j t", t=PACK, j=PACK)
             src = w2_raw[a][:].rearrange("p j (m t) -> p m j t", t=PACK)
-            copy(dst[:, lo:hi], src[:, lo:hi])
+            nc.vector.tensor_copy(dst[:, :, :, t0:t1], src[:, :, :, t0:t1])
 
         def quantize_w2(a, t0, t1):
             nc.vector.quantize_mx(
@@ -187,22 +196,23 @@ def tile_list_tumour_board_page_kernel(
         for t in range(TURNED):
             for h in range(HALVES):
                 make_gain(t, h)
-        for a in range(PASSES):
-            for h in range(HALVES):
-                gather_words(a, h)
+        for h in range(HALVES):
+            gather_words(0, h)
         nc.gpsimd.tensor_copy(
             w1_s[:].rearrange("p a (t m) -> p a t m", t=PACK), w1_s_raw[:].rearrange("p a (m t) -> p a t m", t=PACK)
         )
-        round_w2(nc.vector.tensor_copy, 0, 0, P)
+        round_w2(0, 0, PACK)
         quantize_w2(0, 0, PACK)
-        round_w2(nc.vector.tensor_copy, 1, 0, ROUND_SPLIT)
-        round_w2(nc.scalar.copy, 1, ROUND_SPLIT, P)
+        for h in range(HALVES):
+            gather_words(1, h)
+        round_w2(1, 0, 1)
         quantize_w2(1, 0, 1)
+        round_w2(1, 1, PACK)
         quantize_w2(1, 1, 2)
         quantize_w2(1, 2, PACK)
 
         def square_a(t, h):
-            a_sum = bank("a_sum")
+            a_sum = bank("a_sum", A_BANKS[t][h])
             for a in reversed(range(PASSES)):
                 nc.tensor.matmul_mx(
                     out=a_sum[:],
@@ -215,26 +225,27 @@ def tile_list_tumour_board_page_kernel(
                 )
             nc.scalar.activation(a_sq[t][:, cols(h)], a_sum[:], ACT.Square)
 
-        def square_b(t, h):
-            b_sum = bank("b_sum")
-            order = (0, 1) if t == h == 0 else (1, 0)
+        def square_b(t, h, number, order, lo=0, hi=BANK):
+            b_sum = bank("b_sum", number)
+            j_cols = slice(h * BANK + lo, h * BANK + hi)
             for a in order:
                 nc.tensor.matmul_mx(
-                    out=b_sum[:],
+                    out=b_sum[:, lo:hi],
                     lhsT=w2_w[a][:, cols(t, P)].bitcast(FP8X4),
                     lhsT_scale=w2_s[a][:, cols(t, P)],
-                    rhs=v_w[a][h][:].bitcast(FP8X4),
-                    rhs_scale=v_s[SCALE_ROWS * a :, cols(h)],
+                    rhs=v_w[a][h][:, lo:hi].bitcast(FP8X4),
+                    rhs_scale=v_s[SCALE_ROWS * a :, j_cols],
                     start=(a == order[0]),
                     stop=(a == order[-1]),
                 )
-            nc.scalar.activation(b_sq[t][:, cols(h)], b_sum[:], ACT.Square)
+            nc.scalar.activation(b_sq[t][:, j_cols], b_sum[:, lo:hi], ACT.Square)
 
         def weigh(engine, buffer, t, h):
             diff = held(buffer, [P, BANK], F32)
             engine.tensor_tensor(diff[:], a_sq[t][:, cols(h)], b_sq[t][:, cols(h)], ALU.subtract)
             engine.tensor_tensor(a_sq[t][:, cols(h)], diff[:], gain[t][:, cols(h)], ALU.mult)
 
+        diff_first = held("diff_first", [P, BANK], F32)
         for t in range(EARLY):
             for h in range(HALVES):
                 square_a(t, h)
@@ -242,10 +253,14 @@ def tile_list_tumour_board_page_kernel(
             for h in range(HALVES):
                 if t >= EARLY:
                     square_a(t, h)
-                square_b(t, h)
                 if t == h == 0:
-                    weigh(nc.vector, "diff_first", t, h)
+                    for part in range(2):
+                        j_cols = cols(part, BANK // 2)
+                        square_b(t, h, FIRST_BANKS[part], (0, 1), j_cols.start, j_cols.stop)
+                        nc.vector.tensor_tensor(diff_first[:, j_cols], a_sq[t][:, j_cols], b_sq[t][:, j_cols], ALU.subtract)
+                        nc.vector.tensor_tensor(a_sq[t][:, j_cols], diff_first[:, j_cols], gain_first[:, j_cols], ALU.mult)
                 else:
+                    square_b(t, h, B_BANKS[t][h], (1, 0))
                     weigh(nc.gpsimd, "diff", t, h)
                 nc.vector.tensor_copy(page[t][:].indirect(place[:, cols(h, LIST_COLS)]), a_sq[t][:, cols(h)])
 
@@ -257,11 +272,11 @@ def tile_list_tumour_board_page_kernel(
                     nc.scalar.copy(page_bf[c][:, :, t], page[t][:, cols(c)])
             if t == PACK - 2:
                 for c in range(CHUNKS):
-                    twice = page[t][:, cols(c)].unsqueeze(2).to_broadcast([P, BANK, 2])
                     if c < CHUNKS // 2:
-                        nc.scalar.copy(page_bf[c][:, :, t:], twice)
-                    else:
+                        twice = page[t][:, cols(c)].unsqueeze(2).to_broadcast([P, BANK, 2])
                         nc.gpsimd.tensor_scalar(page_bf[c][:, :, t:], twice, 1.0, 0.0, ALU.mult, ALU.add)
+                    else:
+                        nc.scalar.copy(page_bf[c][:, :, t], page[t][:, cols(c)])
 
         codes_out = out_2[0].rearrange("p m i -> p (m i)").bitcast(I32)
 
@@ -275,45 +290,60 @@ def tile_list_tumour_board_page_kernel(
                 in_=page_bf[c][:].rearrange("p m t -> p (m t)"),
             )
 
-        def store_codes(g):
-            nc.sync.dma_start(codes_out[:, cols(g, PAIR)], page_w[g][:])
+        def store_codes(c0, c1):
+            first = c0 // 2 * PAIR
+            nc.sync.dma_start(codes_out[:, c0 * BANK : c1 * BANK], page_w[c0 // 2][:, c0 * BANK - first : c1 * BANK - first])
 
-        def gate(g, i, widths):
-            sig = ring.tile([P, PAIR], F32, name="sig", bufs=3)
-            for u in range(2):
-                e_sum = bank("e_sum")
-                nc.tensor.matmul_mx(
-                    out=e_sum[:],
-                    lhsT=w3_w[:, cols(i, P)].bitcast(FP8X4),
-                    lhsT_scale=w3_s[:, cols(i, P)],
-                    rhs=page_w[g][:, cols(u)].bitcast(FP8X4),
-                    rhs_scale=page_s[:, cols(2 * g + u)],
-                    start=True,
-                    stop=True,
-                )
-                nc.scalar.activation(sig[:, cols(u)], e_sum[:], ACT.Sigmoid, bias=bias_col[:, i : i + 1])
-            lo = 0
-            for width in widths:
-                m_cols = slice(PAIR * g + lo, PAIR * g + lo + width)
-                nc.vector.tensor_tensor(site_t[i][:, m_cols], sig[:, lo : lo + width], site_t[i][:, m_cols], ALU.mult)
-                nc.sync.dma_start(out_0[cols(i, P), m_cols], site_t[i][:, m_cols])
-                lo = lo + width
+        def gate(n, c, i):
+            sig = ring.tile([P, BANK], F32, name="sig", bufs=6)
+            e_sum = bank("e_sum", n % 8)
+            nc.tensor.matmul_mx(
+                out=e_sum[:],
+                lhsT=w3_w[:, cols(i, P)].bitcast(FP8X4),
+                lhsT_scale=w3_s[:, cols(i, P)],
+                rhs=page_w[c // 2][:, cols(c % 2)].bitcast(FP8X4),
+                rhs_scale=page_s[:, cols(c)],
+                start=True,
+                stop=True,
+            )
+            nc.scalar.activation(sig[:], e_sum[:], ACT.Sigmoid, bias=bias_col[:, i : i + 1])
+            return sig
+
+        def weigh_site(sig, c, i, lo, hi):
+            y = site_t[i][:, BANK * c + lo : BANK * c + hi]
+            nc.vector.tensor_tensor(y, sig[:, lo:hi], y, ALU.mult)
+
+        def store_y(i, lo, hi):
+            nc.sync.dma_start(out_0[cols(i, P), lo:hi], site_t[i][:, lo:hi])
 
         round_last_slice(nc.vector.tensor_copy, 0)
-        round_last_slice(nc.scalar.copy, 1)
         quantize_page(0)
+        store_codes(0, 1)
+        round_last_slice(nc.vector.tensor_copy, 1)
         quantize_page(1)
-        store_codes(0)
-        round_last_slice(nc.vector.tensor_copy, 2)
-        round_last_slice(nc.vector.tensor_copy, 3)
+        store_codes(1, 2)
+        round_last_slice(nc.scalar.copy, 2)
+        round_last_slice(nc.scalar.copy, 3)
         quantize_page(2)
+        store_codes(2, 3)
         quantize_page(3)
-        store_codes(1)
-        for i in range(N_TILES):
-            gate(0, i, (PAIR,))
+        store_codes(3, 4)
         for q in range(QUADS):
             nc.sync.dma_start(
                 out_3[0, cols(q, SCALE_ROWS), :].bitcast(I32), page_s[rows_of(q, SCALE_ROWS), :].bitcast(I32)
             )
-        for i in range(N_TILES):
-            gate(1, i, LAST_WIDTHS if i == N_TILES - 1 else (PAIR,))
+        for c in range(2):
+            for i in range(N_TILES):
+                weigh_site(gate(N_TILES * c + i, c, i), c, i, 0, BANK)
+                store_y(i, BANK * c, BANK * (c + 1))
+        for i in range(N_TILES - 1):
+            for c in range(2, CHUNKS):
+                weigh_site(gate(PAIRED + 2 * i + c, c, i), c, i, 0, BANK)
+            store_y(i, PAIR, T)
+        i = N_TILES - 1
+        weigh_site(gate(PAIRED + 2 * i + 2, 2, i), 2, i, 0, BANK)
+        store_y(i, PAIR, PAIR + BANK)
+        sig = gate(PAIRED + 2 * i + 3, 3, i)
+        for lo in (0, BANK // 2):
+            weigh_site(sig, 3, i, lo, lo + BANK // 2)
+            store_y(i, 3 * BANK + lo, 3 * BANK + lo + BANK // 2)

@@ -29,12 +29,13 @@ LIST_COLS = BANK // 16
 CHUNKS = T // BANK
 PAIR = 2 * BANK
 N_TILES = N // P
-TURNED = 2
+PARKED = 8
+TURNED = 4
 EARLY = 1
 SITE_FIRST = 3
-FIRST_BANKS = (7, 1)
-A_BANKS = ((6, 0), (7, 1), (3, 4), (5, 6))
-B_BANKS = ((None, 3), (4, 5), (6, 0), (7, 1))
+FIRST_BANKS = (3, 4)
+A_BANKS = ((6, 7), (3, 4), (5, 0), (1, 6))
+B_BANKS = ((None, 5), (0, 1), (6, 7), (3, 4))
 LAST_WIDTHS = (512, 256, 256)
 PAIRED = 2 * N_TILES - 2
 
@@ -77,9 +78,7 @@ def tile_list_tumour_board_page_kernel(
         w2_w = [held("w2_w%d" % a, [P, H], U32, tag="shared%d" % (PASSES + a)) for a in range(PASSES)]
         w2_s = [held("w2_s%d" % a, [P, H], U8) for a in range(PASSES)]
         wgs_raw = held("wgs_raw", [P, S], F32)
-        gain_late = held("gain_late", [P, PACK - TURNED, S], F32)
-        gain = [held("gain%d" % t, [P, S], F32) for t in range(TURNED)]
-        gain = gain + [gain_late[:, t, :] for t in range(PACK - TURNED)]
+        gain = [held("gain%d" % t, [P, S], F32) for t in range(PACK)]
         page = [held("page%d" % t, [P, T], F32) for t in range(PACK)]
         a_sq = [held("a_sq%d" % t, [P, S], F32) for t in range(PACK)]
         b_sq = [held("b_sq%d" % t, [P, S], F32) for t in range(PACK)]
@@ -91,7 +90,8 @@ def tile_list_tumour_board_page_kernel(
         page_s = held("page_s", [P, T], U8)
         ident = held("ident", [P, P], F32)
 
-        for scale_tile in (tab_s[:], w1_s_raw[:].rearrange("p a c -> p (a c)"), v_s_low[:], w3_s[:]):
+        nc.gpsimd.memset(tab_s[:].bitcast(I32), 0)
+        for scale_tile in (w1_s_raw[:].rearrange("p a c -> p (a c)"), v_s_low[:], w3_s[:]):
             nc.vector.memset(scale_tile.bitcast(I32), 0)
         make_identity(nc, ident[:])
         warm = held("warm", [P, 1], F32)
@@ -109,20 +109,20 @@ def tile_list_tumour_board_page_kernel(
 
         nc.sync.dma_start(pick[:], offs)
         nc.sync.dma_start(w1_raw[:].bitcast(I32), w1_words.rearrange("a p c -> p a c").bitcast(I32))
+        nc.sync.dma_start(wgs_raw[:], wgs)
         for q in range(QUADS):
             nc.sync.dma_start(
-                tab_s[rows_of(q, SCALE_ROWS * PASSES), :].bitcast(I32),
-                tab_scales[:, cols(q, SCALE_ROWS), :].bitcast(I32),
+                tab_s[rows_of(q, SCALE_ROWS), :].bitcast(I32), tab_scales[0, cols(q, SCALE_ROWS), :].bitcast(I32)
             )
-        nc.sync.dma_start(wgs_raw[:], wgs)
+        nc.sync.dma_start(tab_s[PARKED : PARKED + QUADS * SCALE_ROWS, :].bitcast(I32), tab_scales[1].bitcast(I32))
         load_tab(0)
         for q in range(QUADS):
             nc.sync.dma_start(
                 w1_s_raw[rows_of(q, SCALE_ROWS), :, :].bitcast(I32),
                 w1_scales[:, cols(q, SCALE_ROWS), :].rearrange("a r c -> r a c").bitcast(I32),
             )
-        load_w2(0)
         load_tab(1)
+        load_w2(0)
 
         for a in range(PASSES):
             nc.vector.tensor_copy(
@@ -133,18 +133,13 @@ def tile_list_tumour_board_page_kernel(
         for q in range(QUADS):
             nc.sync.dma_start(
                 v_s_low[rows_of(q, SCALE_ROWS), :].bitcast(I32),
-                v_s[rows_of(q, SCALE_ROWS, first=SCALE_ROWS), :].bitcast(I32),
+                v_s[PARKED + SCALE_ROWS * q : PARKED + SCALE_ROWS * (q + 1), :].bitcast(I32),
             )
 
         load_w2(1)
         nc.sync.dma_start(place[:], offs2)
         nc.sync.dma_start(page[0][:], page_rows[0])
         nc.sync.dma_start(page[1][:], page_rows[1])
-        for q in (0, 2, 1, 3):
-            nc.sync.dma_start(
-                gain_late[rows_of(q, QUAD), :, :], wgs.rearrange("(m t) j -> m t j", t=PACK)[:, TURNED:, :]
-            )
-        nc.sync.dma_start(page[2][:], page_rows[2])
         nc.sync.dma_start(w3_w[:], w3_words[0].rearrange("p c i -> p (c i)").bitcast(I32))
         for q in range(QUADS):
             nc.sync.dma_start(
@@ -154,6 +149,7 @@ def tile_list_tumour_board_page_kernel(
             nc.sync.dma_start(bias_col[:], bias.rearrange("(i p) -> p i", p=P))
         for i in range(N_TILES):
             if i == SITE_FIRST:
+                nc.sync.dma_start(page[2][:], page_rows[2])
                 nc.sync.dma_start(page[3][:], page_rows[3])
             nc.sync.dma_start(site_t[i][:], site[cols(i, P), :])
 
@@ -172,7 +168,7 @@ def tile_list_tumour_board_page_kernel(
                 spread[:].rearrange("p (b q m) -> p b q m", q=QUADS, m=QUAD),
                 picked.unsqueeze(2).to_broadcast([P, BANK // P, QUADS, QUAD]),
             )
-            back = gain_first if t == h == 0 else bank("back", 2 + HALVES * t + h)
+            back = gain_first if t == h == 0 else bank("back", 3 + (HALVES * t + h) % 3)
             for b in range(BANK // P):
                 nc.tensor.transpose(back[:, cols(b, P)], spread[:, cols(b, P)], ident[:])
             if back is not gain_first:
@@ -196,15 +192,14 @@ def tile_list_tumour_board_page_kernel(
         for t in range(TURNED):
             for h in range(HALVES):
                 make_gain(t, h)
-        for h in range(HALVES):
-            gather_words(0, h)
+        for a in range(PASSES):
+            for h in range(HALVES):
+                gather_words(a, h)
         nc.gpsimd.tensor_copy(
             w1_s[:].rearrange("p a (t m) -> p a t m", t=PACK), w1_s_raw[:].rearrange("p a (m t) -> p a t m", t=PACK)
         )
         round_w2(0, 0, PACK)
         quantize_w2(0, 0, PACK)
-        for h in range(HALVES):
-            gather_words(1, h)
         round_w2(1, 0, 1)
         quantize_w2(1, 0, 1)
         round_w2(1, 1, PACK)
@@ -225,18 +220,18 @@ def tile_list_tumour_board_page_kernel(
                 )
             nc.scalar.activation(a_sq[t][:, cols(h)], a_sum[:], ACT.Square)
 
-        def square_b(t, h, number, order, lo=0, hi=BANK):
+        def square_b(t, h, number, lo=0, hi=BANK):
             b_sum = bank("b_sum", number)
             j_cols = slice(h * BANK + lo, h * BANK + hi)
-            for a in order:
+            for a in reversed(range(PASSES)):
                 nc.tensor.matmul_mx(
                     out=b_sum[:, lo:hi],
                     lhsT=w2_w[a][:, cols(t, P)].bitcast(FP8X4),
                     lhsT_scale=w2_s[a][:, cols(t, P)],
                     rhs=v_w[a][h][:, lo:hi].bitcast(FP8X4),
-                    rhs_scale=v_s[SCALE_ROWS * a :, j_cols],
-                    start=(a == order[0]),
-                    stop=(a == order[-1]),
+                    rhs_scale=(v_s, v_s_low)[a][:, j_cols],
+                    start=(a == PASSES - 1),
+                    stop=(a == 0),
                 )
             nc.scalar.activation(b_sq[t][:, j_cols], b_sum[:, lo:hi], ACT.Square)
 
@@ -256,11 +251,11 @@ def tile_list_tumour_board_page_kernel(
                 if t == h == 0:
                     for part in range(2):
                         j_cols = cols(part, BANK // 2)
-                        square_b(t, h, FIRST_BANKS[part], (0, 1), j_cols.start, j_cols.stop)
+                        square_b(t, h, FIRST_BANKS[part], j_cols.start, j_cols.stop)
                         nc.vector.tensor_tensor(diff_first[:, j_cols], a_sq[t][:, j_cols], b_sq[t][:, j_cols], ALU.subtract)
-                        nc.vector.tensor_tensor(a_sq[t][:, j_cols], diff_first[:, j_cols], gain_first[:, j_cols], ALU.mult)
+                    nc.vector.tensor_tensor(a_sq[t][:, cols(h)], diff_first[:], gain_first[:], ALU.mult)
                 else:
-                    square_b(t, h, B_BANKS[t][h], (1, 0))
+                    square_b(t, h, B_BANKS[t][h])
                     weigh(nc.gpsimd, "diff", t, h)
                 nc.vector.tensor_copy(page[t][:].indirect(place[:, cols(h, LIST_COLS)]), a_sq[t][:, cols(h)])
 

@@ -30,12 +30,14 @@ CHUNKS = T // BANK
 PAIR = 2 * BANK
 N_TILES = N // P
 PARKED = 8
-TURNED = 4
-EARLY = 1
+TURNED = 3
+EARLY = 2
+HALVED = 2
 SITE_FIRST = 3
-FIRST_BANKS = (3, 4)
-A_BANKS = ((6, 7), (3, 4), (5, 0), (1, 6))
-B_BANKS = ((None, 5), (0, 1), (6, 7), (3, 4))
+FIRST_BANKS = (4, 6)
+A_BANKS = ((6, 7), (5, 3), (4, 7), (3, 6))
+B_BANKS = ((None, 7), (5, 3), (6, 5), (4, 7))
+BACK_BANKS = ((None, 3), (4, 5), (3, 4), (2, 2))
 LAST_WIDTHS = (512, 256, 256)
 PAIRED = 2 * N_TILES - 2
 
@@ -162,13 +164,16 @@ def tile_list_tumour_board_page_kernel(
             turned.append(first)
 
         def make_gain(t, h):
-            spread = ring.tile([P, BANK], F32, name="spread")
+            if t < TURNED:
+                spread = ring.tile([P, BANK], F32, name="spread")
+            else:
+                spread = held("spread_late", [P, BANK], F32, tag="diff_first")
             picked = turned[h][:].rearrange("p (b m t) -> p t b m", t=PACK, m=QUAD)[:, t]
             nc.scalar.copy(
                 spread[:].rearrange("p (b q m) -> p b q m", q=QUADS, m=QUAD),
                 picked.unsqueeze(2).to_broadcast([P, BANK // P, QUADS, QUAD]),
             )
-            back = gain_first if t == h == 0 else bank("back", 3 + (HALVES * t + h) % 3)
+            back = gain_first if t == h == 0 else bank("back", BACK_BANKS[t][h])
             for b in range(BANK // P):
                 nc.tensor.transpose(back[:, cols(b, P)], spread[:, cols(b, P)], ident[:])
             if back is not gain_first:
@@ -235,10 +240,10 @@ def tile_list_tumour_board_page_kernel(
                 )
             nc.scalar.activation(b_sq[t][:, j_cols], b_sum[:, lo:hi], ACT.Square)
 
-        def weigh(engine, buffer, t, h):
-            diff = held(buffer, [P, BANK], F32)
-            engine.tensor_tensor(diff[:], a_sq[t][:, cols(h)], b_sq[t][:, cols(h)], ALU.subtract)
-            engine.tensor_tensor(a_sq[t][:, cols(h)], diff[:], gain[t][:, cols(h)], ALU.mult)
+        def weigh(t, j_cols):
+            diff = held("diff", [P, S], F32)
+            nc.gpsimd.tensor_tensor(diff[:, j_cols], a_sq[t][:, j_cols], b_sq[t][:, j_cols], ALU.subtract)
+            nc.gpsimd.tensor_tensor(a_sq[t][:, j_cols], diff[:, j_cols], gain[t][:, j_cols], ALU.mult)
 
         diff_first = held("diff_first", [P, BANK], F32)
         for t in range(EARLY):
@@ -246,6 +251,8 @@ def tile_list_tumour_board_page_kernel(
                 square_a(t, h)
         for t in range(PACK):
             for h in range(HALVES):
+                if t >= TURNED:
+                    make_gain(t, h)
                 if t >= EARLY:
                     square_a(t, h)
                 if t == h == 0:
@@ -256,8 +263,13 @@ def tile_list_tumour_board_page_kernel(
                     nc.vector.tensor_tensor(a_sq[t][:, cols(h)], diff_first[:], gain_first[:], ALU.mult)
                 else:
                     square_b(t, h, B_BANKS[t][h])
-                    weigh(nc.gpsimd, "diff", t, h)
-                nc.vector.tensor_copy(page[t][:].indirect(place[:, cols(h, LIST_COLS)]), a_sq[t][:, cols(h)])
+                    if t < HALVED:
+                        weigh(t, cols(h))
+                if t < HALVED:
+                    nc.vector.tensor_copy(page[t][:].indirect(place[:, cols(h, LIST_COLS)]), a_sq[t][:, cols(h)])
+            if t >= HALVED:
+                weigh(t, slice(0, S))
+                nc.vector.tensor_copy(page[t][:].indirect(place[:]), a_sq[t][:])
 
         page_bf = [held("page_bf%d" % c, [P, BANK, PACK], BF16, tag="shared%d" % c) for c in range(CHUNKS)]
         for t in range(PACK):
@@ -268,8 +280,10 @@ def tile_list_tumour_board_page_kernel(
             if t == PACK - 2:
                 for c in range(CHUNKS):
                     if c < CHUNKS // 2:
-                        twice = page[t][:, cols(c)].unsqueeze(2).to_broadcast([P, BANK, 2])
-                        nc.gpsimd.tensor_scalar(page_bf[c][:, :, t:], twice, 1.0, 0.0, ALU.mult, ALU.add)
+                        src = page[t][:, cols(c)]
+                        nc.gpsimd.tensor_scalar(page_bf[c][:, 2:, t], src[:, 2:], 1.0, 0.0, ALU.mult, ALU.add)
+                        twice = src[:, 0:2].unsqueeze(2).to_broadcast([P, 2, 2])
+                        nc.gpsimd.tensor_scalar(page_bf[c][:, 0:2, t:], twice, 1.0, 0.0, ALU.mult, ALU.add)
                     else:
                         nc.scalar.copy(page_bf[c][:, :, t], page[t][:, cols(c)])
 

@@ -205,10 +205,10 @@ def tile_list_tumour_board_page_kernel(
         )
         round_w2(0, 0, PACK)
         quantize_w2(0, 0, PACK)
-        round_w2(1, 0, 1)
+        round_w2(1, 0, 2)
         quantize_w2(1, 0, 1)
-        round_w2(1, 1, PACK)
         quantize_w2(1, 1, 2)
+        round_w2(1, 2, PACK)
         quantize_w2(1, 2, PACK)
 
         def square_a(t, h):
@@ -348,7 +348,7 @@ def tile_list_tumour_board_page_kernel(
         for i in range(N_TILES - 1):
             for c in range(2, CHUNKS):
                 weigh_site(gate(PAIRED + 2 * i + c, c, i), c, i, 0, BANK)
-            store_y(i, PAIR, T)
+                store_y(i, BANK * c, BANK * (c + 1))
         i = N_TILES - 1
         weigh_site(gate(PAIRED + 2 * i + 2, 2, i), 2, i, 0, BANK)
         store_y(i, PAIR, PAIR + BANK)

@@ -36,7 +36,7 @@ HALVED = 2
 SITE_FIRST = 3
 FIRST_BANKS = (4, 6)
 A_BANKS = ((6, 7), (5, 3), (4, 7), (3, 6))
-B_BANKS = ((None, 7), (5, 3), (6, 5), (4, 7))
+B_BANKS = ((None, 5), (7, 3), (6, 5), (4, 7))
 BACK_BANKS = ((None, 3), (4, 5), (3, 4), (2, 2))
 LAST_WIDTHS = (512, 256, 256)
 PAIRED = 2 * N_TILES - 2
@@ -249,25 +249,26 @@ def tile_list_tumour_board_page_kernel(
         for t in range(EARLY):
             for h in range(HALVES):
                 square_a(t, h)
-        for t in range(PACK):
-            for h in range(HALVES):
-                if t >= TURNED:
-                    make_gain(t, h)
-                if t >= EARLY:
-                    square_a(t, h)
-                if t == h == 0:
-                    for part in range(2):
-                        j_cols = cols(part, BANK // 2)
-                        square_b(t, h, FIRST_BANKS[part], j_cols.start, j_cols.stop)
-                        nc.vector.tensor_tensor(diff_first[:, j_cols], a_sq[t][:, j_cols], b_sq[t][:, j_cols], ALU.subtract)
-                    nc.vector.tensor_tensor(a_sq[t][:, cols(h)], diff_first[:], gain_first[:], ALU.mult)
-                else:
-                    square_b(t, h, B_BANKS[t][h])
-                    if t < HALVED:
-                        weigh(t, cols(h))
+        pieces = [(t, h) for h in range(HALVES) for t in range(HALVED)]
+        pieces = pieces + [(t, h) for t in range(HALVED, PACK) for h in range(HALVES)]
+        for t, h in pieces:
+            if t >= TURNED:
+                make_gain(t, h)
+            if t >= EARLY:
+                square_a(t, h)
+            if t == h == 0:
+                for part in range(2):
+                    j_cols = cols(part, BANK // 2)
+                    square_b(t, h, FIRST_BANKS[part], j_cols.start, j_cols.stop)
+                    nc.vector.tensor_tensor(diff_first[:, j_cols], a_sq[t][:, j_cols], b_sq[t][:, j_cols], ALU.subtract)
+                nc.vector.tensor_tensor(a_sq[t][:, cols(h)], diff_first[:], gain_first[:], ALU.mult)
+            else:
+                square_b(t, h, B_BANKS[t][h])
                 if t < HALVED:
-                    nc.vector.tensor_copy(page[t][:].indirect(place[:, cols(h, LIST_COLS)]), a_sq[t][:, cols(h)])
-            if t >= HALVED:
+                    weigh(t, cols(h))
+            if t < HALVED:
+                nc.vector.tensor_copy(page[t][:].indirect(place[:, cols(h, LIST_COLS)]), a_sq[t][:, cols(h)])
+            elif h == HALVES - 1:
                 weigh(t, slice(0, S))
                 nc.vector.tensor_copy(page[t][:].indirect(place[:]), a_sq[t][:])
 

@@ -29,15 +29,14 @@ LIST_COLS = BANK // 16
 CHUNKS = T // BANK
 PAIR = 2 * BANK
 N_TILES = N // P
-PARKED = 8
-TURNED = 3
-EARLY = 2
+QUARTER = BANK // 2
 HALVED = 2
 SITE_FIRST = 3
-FIRST_BANKS = (4, 6)
-A_BANKS = ((6, 7), (5, 3), (4, 7), (3, 6))
-B_BANKS = ((None, 5), (7, 3), (6, 5), (4, 7))
-BACK_BANKS = ((None, 3), (4, 5), (3, 4), (2, 2))
+FIRST_BANKS = (5, 6, 7, 1)
+SUM_BANKS = (3, 4, 6, 0) + 2 * (7, 1, 4, 6, 0)
+TURN_BANKS = (0, 3)
+BACK_BANKS = ((4, 3), (2, 5))
+PAGE_BF_ON = ("tab_w0", "tab_w1", "w2_raw0", "w2_raw1")
 LAST_WIDTHS = (512, 256, 256)
 PAIRED = 2 * N_TILES - 2
 
@@ -68,9 +67,10 @@ def tile_list_tumour_board_page_kernel(
         place = keep.tile([P, S // 16], U16, name="place")
         tab_w = [held("tab_w%d" % a, [P, T], I32) for a in range(PASSES)]
         tab_s = held("tab_s", [P, T], U8)
-        v_w = [[held("v_w%d_%d" % (a, h), [P, BANK], U32) for h in range(HALVES)] for a in range(PASSES)]
-        v_s = held("v_s", [P, S], U8)
-        v_s_low = held("v_s_low", [P, S], U8)
+        runs = (((0, BANK), (BANK, S)), ((0, QUARTER), (QUARTER, BANK), (BANK, S)))
+        v_w = [[held("v_w%d_%d" % (a, lo), [P, hi - lo], U32) for lo, hi in runs[a]] for a in range(PASSES)]
+        v_s_rows = held("v_s_rows", [P, S], U8)
+        v_s = [held("v_s%d" % a, [P, S], U8) for a in range(PASSES)]
         w1_raw = held("w1_raw", [P, PASSES, 2 * H], U8)
         w1_s_raw = held("w1_s_raw", [P, PASSES, H], U8)
         w1_w = [held("w1_w%d" % a, [P, 2 * H], U8, tag="shared%d" % a) for a in range(PASSES)]
@@ -79,7 +79,7 @@ def tile_list_tumour_board_page_kernel(
         w2_bf = [held("w2_bf%d" % a, [P, PACK * H], BF16) for a in range(PASSES)]
         w2_w = [held("w2_w%d" % a, [P, H], U32, tag="shared%d" % (PASSES + a)) for a in range(PASSES)]
         w2_s = [held("w2_s%d" % a, [P, H], U8) for a in range(PASSES)]
-        wgs_raw = held("wgs_raw", [P, S], F32)
+        wgs_raw = [held("wgs_raw%d" % h, [P, BANK], F32) for h in range(HALVES)]
         gain = [held("gain%d" % t, [P, S], F32) for t in range(PACK)]
         page = [held("page%d" % t, [P, T], F32) for t in range(PACK)]
         a_sq = [held("a_sq%d" % t, [P, S], F32) for t in range(PACK)]
@@ -92,8 +92,9 @@ def tile_list_tumour_board_page_kernel(
         page_s = held("page_s", [P, T], U8)
         ident = held("ident", [P, P], F32)
 
-        nc.gpsimd.memset(tab_s[:].bitcast(I32), 0)
-        for scale_tile in (w1_s_raw[:].rearrange("p a c -> p (a c)"), v_s_low[:], w3_s[:]):
+        nc.vector.memset(tab_s[QUAD : 2 * QUAD, :].bitcast(I32), 0)
+        nc.vector.memset(tab_s[2 * QUAD :, :].bitcast(I32), 0)
+        for scale_tile in (w1_s_raw[:].rearrange("p a c -> p (a c)"), v_s[0][:], v_s[1][:], w3_s[:]):
             nc.vector.memset(scale_tile.bitcast(I32), 0)
         make_identity(nc, ident[:])
         warm = held("warm", [P, 1], F32)
@@ -109,39 +110,35 @@ def tile_list_tumour_board_page_kernel(
             k_rows = w2[cols(a, P * PACK), :]
             nc.sync.dma_start(w2_raw[a][:], k_rows.rearrange("(p j) c -> p j c", j=PACK))
 
+        def move_scale_rows(a):
+            for q in range(QUADS):
+                first = QUADS * SCALE_ROWS * a + SCALE_ROWS * q
+                nc.sync.dma_start(
+                    v_s[a][rows_of(q, SCALE_ROWS), :].bitcast(I32), v_s_rows[first : first + SCALE_ROWS, :].bitcast(I32)
+                )
+
+        nc.sync.dma_start(tab_s[0:QUAD, :].bitcast(I32), tab_scales.rearrange("a q t -> (a q) t").bitcast(I32))
         nc.sync.dma_start(pick[:], offs)
-        nc.sync.dma_start(w1_raw[:].bitcast(I32), w1_words.rearrange("a p c -> p a c").bitcast(I32))
-        nc.sync.dma_start(wgs_raw[:], wgs)
-        for q in range(QUADS):
-            nc.sync.dma_start(
-                tab_s[rows_of(q, SCALE_ROWS), :].bitcast(I32), tab_scales[0, cols(q, SCALE_ROWS), :].bitcast(I32)
-            )
-        nc.sync.dma_start(tab_s[PARKED : PARKED + QUADS * SCALE_ROWS, :].bitcast(I32), tab_scales[1].bitcast(I32))
+        nc.sync.dma_start(wgs_raw[0][:], wgs[:, cols(0)])
         load_tab(0)
         for q in range(QUADS):
             nc.sync.dma_start(
                 w1_s_raw[rows_of(q, SCALE_ROWS), :, :].bitcast(I32),
                 w1_scales[:, cols(q, SCALE_ROWS), :].rearrange("a r c -> r a c").bitcast(I32),
             )
-        load_tab(1)
         load_w2(0)
-
-        for a in range(PASSES):
-            nc.vector.tensor_copy(
-                w1_w[a][:].bitcast(U16).rearrange("p (t m) -> p m t", t=PACK),
-                w1_raw[:, a, :].bitcast(U16).rearrange("p (m t) -> p m t", t=PACK),
-            )
-        nc.vector.tensor_copy(v_s[:], tab_s[:].indirect(pick[:]))
-        for q in range(QUADS):
-            nc.sync.dma_start(
-                v_s_low[rows_of(q, SCALE_ROWS), :].bitcast(I32),
-                v_s[PARKED + SCALE_ROWS * q : PARKED + SCALE_ROWS * (q + 1), :].bitcast(I32),
-            )
-
         load_w2(1)
+        nc.vector.tensor_copy(v_s_rows[:], tab_s[:].indirect(pick[:]))
+        move_scale_rows(0)
+        nc.sync.dma_start(w1_raw[:].bitcast(I32), w1_words.rearrange("a p c -> p a c").bitcast(I32))
+        load_tab(1)
+        move_scale_rows(1)
         nc.sync.dma_start(place[:], offs2)
+        nc.sync.dma_start(wgs_raw[1][:], wgs[:, cols(1)])
         nc.sync.dma_start(page[0][:], page_rows[0])
         nc.sync.dma_start(page[1][:], page_rows[1])
+        for q in range(QUADS):
+            nc.sync.dma_start(gain[0][rows_of(q, QUAD), cols(1)], wgs.rearrange("(m t) j -> t m j", t=PACK)[0, :, cols(1)])
         nc.sync.dma_start(w3_w[:], w3_words[0].rearrange("p c i -> p (c i)").bitcast(I32))
         for q in range(QUADS):
             nc.sync.dma_start(
@@ -157,136 +154,143 @@ def tile_list_tumour_board_page_kernel(
 
         gain_first = bank("gain_first", 2)
         turned = []
-        for h in range(HALVES):
-            first = bank("turned%d" % h, h)
+
+        def turn(h):
+            first = bank("turned%d" % h, TURN_BANKS[h])
             for b in range(BANK // P):
-                nc.tensor.transpose(first[:, cols(b, P)], wgs_raw[:, cols(h * (BANK // P) + b, P)], ident[:])
+                nc.tensor.transpose(first[:, cols(b, P)], wgs_raw[h][:, cols(b, P)], ident[:])
             turned.append(first)
 
         def make_gain(t, h):
-            if t < TURNED:
-                spread = ring.tile([P, BANK], F32, name="spread")
-            else:
-                spread = held("spread_late", [P, BANK], F32, tag="diff_first")
+            spread = ring.tile([P, BANK], F32, name="spread")
             picked = turned[h][:].rearrange("p (b m t) -> p t b m", t=PACK, m=QUAD)[:, t]
             nc.scalar.copy(
                 spread[:].rearrange("p (b q m) -> p b q m", q=QUADS, m=QUAD),
                 picked.unsqueeze(2).to_broadcast([P, BANK // P, QUADS, QUAD]),
             )
-            back = gain_first if t == h == 0 else bank("back", BACK_BANKS[t][h])
+            back = gain_first if t == h == 0 else bank("back", BACK_BANKS[h][t % 2])
             for b in range(BANK // P):
                 nc.tensor.transpose(back[:, cols(b, P)], spread[:, cols(b, P)], ident[:])
             if back is not gain_first:
                 nc.scalar.copy(gain[t][:, cols(h)], back[:])
 
-        def gather_words(a, h):
-            nc.vector.tensor_copy(v_w[a][h][:], tab_w[a][:].bitcast(U32).indirect(pick[:, cols(h, LIST_COLS)]))
+        turn(0)
+        for t in range(PACK):
+            make_gain(t, 0)
 
-        def round_w2(a, t0, t1):
-            dst = w2_bf[a][:].rearrange("p (t m j) -> p m j t", t=PACK, j=PACK)
-            src = w2_raw[a][:].rearrange("p j (m t) -> p m j t", t=PACK)
-            nc.vector.tensor_copy(dst[:, :, :, t0:t1], src[:, :, :, t0:t1])
+        def gather_words(a):
+            for words, (lo, hi) in zip(v_w[a], runs[a]):
+                nc.vector.tensor_copy(words[:], tab_w[a][:].bitcast(U32).indirect(pick[:, lo // 16 : hi // 16]))
 
-        def quantize_w2(a, t0, t1):
-            nc.vector.quantize_mx(
-                out=w2_w[a][:, t0 * P : t1 * P].bitcast(FP8X4),
-                scales=w2_s[a][:, t0 * P : t1 * P],
-                in_=w2_bf[a][:, t0 * BANK : t1 * BANK],
-            )
-
-        for t in range(TURNED):
-            for h in range(HALVES):
-                make_gain(t, h)
+        gather_words(0)
         for a in range(PASSES):
-            for h in range(HALVES):
-                gather_words(a, h)
+            nc.vector.tensor_copy(
+                w2_bf[a][:].rearrange("p (t m j) -> p m j t", t=PACK, j=PACK),
+                w2_raw[a][:].rearrange("p j (m t) -> p m j t", t=PACK),
+            )
+            nc.vector.quantize_mx(out=w2_w[a][:].bitcast(FP8X4), scales=w2_s[a][:], in_=w2_bf[a][:])
+        for a in range(PASSES):
+            nc.vector.tensor_copy(
+                w1_w[a][:].bitcast(U16).rearrange("p (t m) -> p m t", t=PACK),
+                w1_raw[:, a, :].bitcast(U16).rearrange("p (m t) -> p m t", t=PACK),
+            )
         nc.gpsimd.tensor_copy(
             w1_s[:].rearrange("p a (t m) -> p a t m", t=PACK), w1_s_raw[:].rearrange("p a (m t) -> p a t m", t=PACK)
         )
-        round_w2(0, 0, PACK)
-        quantize_w2(0, 0, PACK)
-        round_w2(1, 0, 2)
-        quantize_w2(1, 0, 1)
-        quantize_w2(1, 1, 2)
-        round_w2(1, 2, PACK)
-        quantize_w2(1, 2, PACK)
+        gather_words(1)
 
-        def square_a(t, h):
-            a_sum = bank("a_sum", A_BANKS[t][h])
-            for a in reversed(range(PASSES)):
+        def square(squares, number, lo, hi, weights, scales):
+            total = bank("total", number)
+            steps = []
+            for a in range(PASSES):
+                for words, (first, last) in zip(v_w[a], runs[a]):
+                    if first < hi and lo < last:
+                        steps.append((a, words, first, max(lo, first), min(hi, last)))
+            for n, (a, words, first, j0, j1) in enumerate(steps):
                 nc.tensor.matmul_mx(
-                    out=a_sum[:],
-                    lhsT=w1_w[a][:, cols(t, 2 * P)].bitcast(FP4X4),
-                    lhsT_scale=w1_s[:, a, cols(t, P)],
-                    rhs=v_w[a][h][:].bitcast(FP8X4),
-                    rhs_scale=(v_s, v_s_low)[a][:, cols(h)],
-                    start=(a == PASSES - 1),
-                    stop=(a == 0),
+                    out=total[:, j0 - lo : j1 - lo],
+                    lhsT=weights[a],
+                    lhsT_scale=scales[a],
+                    rhs=words[:, j0 - first : j1 - first].bitcast(FP8X4),
+                    rhs_scale=v_s[a][:, j0:j1],
+                    start=(n == 0),
+                    stop=(n == len(steps) - 1),
                 )
-            nc.scalar.activation(a_sq[t][:, cols(h)], a_sum[:], ACT.Square)
+            nc.scalar.activation(squares[:, lo:hi], total[:, : hi - lo], ACT.Square)
 
-        def square_b(t, h, number, lo=0, hi=BANK):
-            b_sum = bank("b_sum", number)
-            j_cols = slice(h * BANK + lo, h * BANK + hi)
-            for a in reversed(range(PASSES)):
-                nc.tensor.matmul_mx(
-                    out=b_sum[:, lo:hi],
-                    lhsT=w2_w[a][:, cols(t, P)].bitcast(FP8X4),
-                    lhsT_scale=w2_s[a][:, cols(t, P)],
-                    rhs=v_w[a][h][:, lo:hi].bitcast(FP8X4),
-                    rhs_scale=(v_s, v_s_low)[a][:, j_cols],
-                    start=(a == PASSES - 1),
-                    stop=(a == 0),
-                )
-            nc.scalar.activation(b_sq[t][:, j_cols], b_sum[:, lo:hi], ACT.Square)
+        def square_a(t, number, lo, hi):
+            weights = [w1_w[a][:, cols(t, 2 * P)].bitcast(FP4X4) for a in range(PASSES)]
+            square(a_sq[t], number, lo, hi, weights, [w1_s[:, a, cols(t, P)] for a in range(PASSES)])
 
-        def weigh(t, j_cols):
+        def square_b(t, number, lo, hi):
+            weights = [w2_w[a][:, cols(t, P)].bitcast(FP8X4) for a in range(PASSES)]
+            square(b_sq[t], number, lo, hi, weights, [w2_s[a][:, cols(t, P)] for a in range(PASSES)])
+
+        def weigh(t, *parts):
             diff = held("diff", [P, S], F32)
-            nc.gpsimd.tensor_tensor(diff[:, j_cols], a_sq[t][:, j_cols], b_sq[t][:, j_cols], ALU.subtract)
-            nc.gpsimd.tensor_tensor(a_sq[t][:, j_cols], diff[:, j_cols], gain[t][:, j_cols], ALU.mult)
+            for j_cols in parts:
+                nc.gpsimd.tensor_tensor(diff[:, j_cols], a_sq[t][:, j_cols], b_sq[t][:, j_cols], ALU.subtract)
+            for j_cols in parts:
+                nc.gpsimd.tensor_tensor(a_sq[t][:, j_cols], diff[:, j_cols], gain[t][:, j_cols], ALU.mult)
 
         diff_first = held("diff_first", [P, BANK], F32)
-        for t in range(EARLY):
-            for h in range(HALVES):
-                square_a(t, h)
         pieces = [(t, h) for h in range(HALVES) for t in range(HALVED)]
         pieces = pieces + [(t, h) for t in range(HALVED, PACK) for h in range(HALVES)]
+        sums = 0
         for t, h in pieces:
-            if t >= TURNED:
+            if h > 0 and t == 0:
+                turn(h)
+            if h > 0 and t > 0:
                 make_gain(t, h)
-            if t >= EARLY:
-                square_a(t, h)
             if t == h == 0:
-                for part in range(2):
-                    j_cols = cols(part, BANK // 2)
-                    square_b(t, h, FIRST_BANKS[part], j_cols.start, j_cols.stop)
-                    nc.vector.tensor_tensor(diff_first[:, j_cols], a_sq[t][:, j_cols], b_sq[t][:, j_cols], ALU.subtract)
+                for lo in range(0, BANK, QUARTER):
+                    hi = lo + QUARTER
+                    square_a(t, FIRST_BANKS[2 * lo // QUARTER], lo, hi)
+                    square_b(t, FIRST_BANKS[2 * lo // QUARTER + 1], lo, hi)
+                    nc.vector.tensor_tensor(diff_first[:, lo:hi], a_sq[t][:, lo:hi], b_sq[t][:, lo:hi], ALU.subtract)
                 nc.vector.tensor_tensor(a_sq[t][:, cols(h)], diff_first[:], gain_first[:], ALU.mult)
             else:
-                square_b(t, h, B_BANKS[t][h])
+                square_a(t, SUM_BANKS[sums], h * BANK, (h + 1) * BANK)
+                square_b(t, SUM_BANKS[sums + 1], h * BANK, (h + 1) * BANK)
+                sums = sums + 2
                 if t < HALVED:
                     weigh(t, cols(h))
             if t < HALVED:
                 nc.vector.tensor_copy(page[t][:].indirect(place[:, cols(h, LIST_COLS)]), a_sq[t][:, cols(h)])
             elif h == HALVES - 1:
-                weigh(t, slice(0, S))
+                if t == PACK - 1:
+                    weigh(t, cols(0), cols(1))
+                else:
+                    weigh(t, slice(0, S))
                 nc.vector.tensor_copy(page[t][:].indirect(place[:]), a_sq[t][:])
 
-        page_bf = [held("page_bf%d" % c, [P, BANK, PACK], BF16, tag="shared%d" % c) for c in range(CHUNKS)]
+        early = PACK - 1
+        rounded = held("rounded", [P, early, T], BF16, tag="shared%d" % (2 * PASSES - 1))
+        page_bf = [held("page_bf%d" % c, [P, BANK, PACK], BF16, tag=PAGE_BF_ON[c]) for c in range(CHUNKS)]
+
+        def pool_copy(dst, src):
+            nc.gpsimd.tensor_scalar(dst, src, 1.0, 0.0, ALU.mult, ALU.add)
+
+        def weave(c, count):
+            dst = page_bf[c][:].rearrange("p (g i) t -> p g t i", i=4)[:, :, 0:count, :]
+            nc.scalar.copy(dst, rounded[:, 0:count, cols(c)].rearrange("p t (g i) -> p g t i", i=4))
+
         for t in range(PACK):
             nc.sync.dma_start(out_rows[t], page[t][:])
-            if t < PACK - 2:
-                for c in range(CHUNKS):
-                    nc.scalar.copy(page_bf[c][:, :, t], page[t][:, cols(c)])
-            if t == PACK - 2:
+            if t < early - 1:
+                nc.scalar.copy(rounded[:, t, :], page[t][:])
+            if t == early - 2:
+                for c in range(CHUNKS // 2):
+                    weave(c, t + 1)
+            if t == early - 1:
+                nc.scalar.copy(rounded[:, t, PAIR:], page[t][:, PAIR:])
                 for c in range(CHUNKS):
                     if c < CHUNKS // 2:
                         src = page[t][:, cols(c)]
-                        nc.gpsimd.tensor_scalar(page_bf[c][:, 2:, t], src[:, 2:], 1.0, 0.0, ALU.mult, ALU.add)
-                        twice = src[:, 0:2].unsqueeze(2).to_broadcast([P, 2, 2])
-                        nc.gpsimd.tensor_scalar(page_bf[c][:, 0:2, t:], twice, 1.0, 0.0, ALU.mult, ALU.add)
+                        pool_copy(page_bf[c][:, 2:, t], src[:, 2:])
+                        pool_copy(page_bf[c][:, 0:2, t:], src[:, 0:2].unsqueeze(2).to_broadcast([P, 2, 2]))
                     else:
-                        nc.scalar.copy(page_bf[c][:, :, t], page[t][:, cols(c)])
+                        weave(c, t + 1)
 
         codes_out = out_2[0].rearrange("p m i -> p (m i)").bitcast(I32)
 

@@ -33,9 +33,9 @@ QUARTER = BANK // 2
 HALVED = 2
 SITE_FIRST = 3
 FIRST_BANKS = (5, 6, 7, 1)
-SUM_BANKS = (3, 4, 6, 0) + 2 * (7, 1, 4, 6, 0)
+SUM_BANKS = ((None, (6, 0)), ((3, 4), (7, 1)), ((4, 6), (2, 5)), ((2, 5), (2, 5)))
 TURN_BANKS = (0, 3)
-BACK_BANKS = ((4, 3), (2, 5))
+BACK_BANKS = ((None, 3, 4, 3), (2, 5, 0, 2))
 PAGE_BF_ON = ("tab_w0", "tab_w1", "w2_raw0", "w2_raw1")
 LAST_WIDTHS = (512, 256, 256)
 PAIRED = 2 * N_TILES - 2
@@ -86,8 +86,10 @@ def tile_list_tumour_board_page_kernel(
         b_sq = [held("b_sq%d" % t, [P, S], F32) for t in range(PACK)]
         w3_w = held("w3_w", [P, N], I32)
         w3_s = held("w3_s", [P, N], U8)
+        bias_rows = held("bias_rows", [P, P], F32)
         bias_col = held("bias_col", [P, N_TILES], F32)
-        site_t = [held("site%d" % i, [P, T], F32) for i in range(N_TILES)]
+        site_parts = (held("site_first", [P, SITE_FIRST, T], F32), held("site_rest", [P, N_TILES - SITE_FIRST, T], F32))
+        site_t = [site_parts[i // SITE_FIRST][:, i % SITE_FIRST, :] for i in range(N_TILES)]
         page_w = [held("page_w%d" % g, [P, PAIR], I32) for g in range(CHUNKS // 2)]
         page_s = held("page_s", [P, T], U8)
         ident = held("ident", [P, P], F32)
@@ -97,6 +99,7 @@ def tile_list_tumour_board_page_kernel(
         for scale_tile in (w1_s_raw[:].rearrange("p a c -> p (a c)"), v_s[0][:], v_s[1][:], w3_s[:]):
             nc.vector.memset(scale_tile.bitcast(I32), 0)
         make_identity(nc, ident[:])
+        nc.gpsimd.memset(bias_rows[:], 0.0)
         warm = held("warm", [P, 1], F32)
         nc.scalar.activation(warm[:], ident[:, 0:1], ACT.Sigmoid)
 
@@ -134,23 +137,20 @@ def tile_list_tumour_board_page_kernel(
         load_tab(1)
         move_scale_rows(1)
         nc.sync.dma_start(place[:], offs2)
-        nc.sync.dma_start(wgs_raw[1][:], wgs[:, cols(1)])
         nc.sync.dma_start(page[0][:], page_rows[0])
         nc.sync.dma_start(page[1][:], page_rows[1])
-        for q in range(QUADS):
-            nc.sync.dma_start(gain[0][rows_of(q, QUAD), cols(1)], wgs.rearrange("(m t) j -> t m j", t=PACK)[0, :, cols(1)])
+        nc.sync.dma_start(wgs_raw[1][:], wgs[:, cols(1)])
         nc.sync.dma_start(w3_w[:], w3_words[0].rearrange("p c i -> p (c i)").bitcast(I32))
         for q in range(QUADS):
             nc.sync.dma_start(
                 w3_s[rows_of(q, SCALE_ROWS), :].bitcast(I32), w3_scales[0, cols(q, SCALE_ROWS), :].bitcast(I32)
             )
-        with nc.allow_non_contiguous_dma(reason="one bias value a partition"):
-            nc.sync.dma_start(bias_col[:], bias.rearrange("(i p) -> p i", p=P))
-        for i in range(N_TILES):
-            if i == SITE_FIRST:
-                nc.sync.dma_start(page[2][:], page_rows[2])
-                nc.sync.dma_start(page[3][:], page_rows[3])
-            nc.sync.dma_start(site_t[i][:], site[cols(i, P), :])
+        nc.sync.dma_start(bias_rows[0:N_TILES, :], bias.rearrange("(i p) -> i p", p=P))
+        site_rows = site.rearrange("(i p) m -> p i m", p=P)
+        nc.sync.dma_start(site_parts[0][:], site_rows[:, :SITE_FIRST, :])
+        nc.sync.dma_start(page[2][:], page_rows[2])
+        nc.sync.dma_start(page[3][:], page_rows[3])
+        nc.sync.dma_start(site_parts[1][:], site_rows[:, SITE_FIRST:, :])
 
         gain_first = bank("gain_first", 2)
         turned = []
@@ -168,7 +168,7 @@ def tile_list_tumour_board_page_kernel(
                 spread[:].rearrange("p (b q m) -> p b q m", q=QUADS, m=QUAD),
                 picked.unsqueeze(2).to_broadcast([P, BANK // P, QUADS, QUAD]),
             )
-            back = gain_first if t == h == 0 else bank("back", BACK_BANKS[h][t % 2])
+            back = gain_first if t == h == 0 else bank("back", BACK_BANKS[h][t])
             for b in range(BANK // P):
                 nc.tensor.transpose(back[:, cols(b, P)], spread[:, cols(b, P)], ident[:])
             if back is not gain_first:
@@ -226,43 +226,55 @@ def tile_list_tumour_board_page_kernel(
             weights = [w2_w[a][:, cols(t, P)].bitcast(FP8X4) for a in range(PASSES)]
             square(b_sq[t], number, lo, hi, weights, [w2_s[a][:, cols(t, P)] for a in range(PASSES)])
 
-        def weigh(t, *parts):
+        def weigh(*parts):
             diff = held("diff", [P, S], F32)
-            for j_cols in parts:
-                nc.gpsimd.tensor_tensor(diff[:, j_cols], a_sq[t][:, j_cols], b_sq[t][:, j_cols], ALU.subtract)
-            for j_cols in parts:
-                nc.gpsimd.tensor_tensor(a_sq[t][:, j_cols], diff[:, j_cols], gain[t][:, j_cols], ALU.mult)
+            room = 0
+            places = []
+            for t, lo, hi in parts:
+                places.append(diff[:, room : room + hi - lo])
+                room = room + hi - lo
+                nc.gpsimd.tensor_tensor(places[-1], a_sq[t][:, lo:hi], b_sq[t][:, lo:hi], ALU.subtract)
+            for (t, lo, hi), place_of_diff in zip(parts, places):
+                nc.gpsimd.tensor_tensor(a_sq[t][:, lo:hi], place_of_diff, gain[t][:, lo:hi], ALU.mult)
 
-        diff_first = held("diff_first", [P, BANK], F32)
-        pieces = [(t, h) for h in range(HALVES) for t in range(HALVED)]
-        pieces = pieces + [(t, h) for t in range(HALVED, PACK) for h in range(HALVES)]
-        sums = 0
-        for t, h in pieces:
-            if h > 0 and t == 0:
-                turn(h)
-            if h > 0 and t > 0:
-                make_gain(t, h)
-            if t == h == 0:
-                for lo in range(0, BANK, QUARTER):
-                    hi = lo + QUARTER
-                    square_a(t, FIRST_BANKS[2 * lo // QUARTER], lo, hi)
-                    square_b(t, FIRST_BANKS[2 * lo // QUARTER + 1], lo, hi)
-                    nc.vector.tensor_tensor(diff_first[:, lo:hi], a_sq[t][:, lo:hi], b_sq[t][:, lo:hi], ALU.subtract)
-                nc.vector.tensor_tensor(a_sq[t][:, cols(h)], diff_first[:], gain_first[:], ALU.mult)
+        def squares(t, h):
+            square_a(t, SUM_BANKS[t][h][0], h * BANK, (h + 1) * BANK)
+            square_b(t, SUM_BANKS[t][h][1], h * BANK, (h + 1) * BANK)
+
+        def scatter(t, lo, hi):
+            nc.vector.tensor_copy(page[t][:].indirect(place[:, lo // 16 : hi // 16]), a_sq[t][:, lo:hi])
+
+        diff_first = held("diff_first", [P, BANK], F32, tag="w2_bf0")
+        for lo in range(0, BANK, QUARTER):
+            hi = lo + QUARTER
+            square_a(0, FIRST_BANKS[2 * lo // QUARTER], lo, hi)
+            square_b(0, FIRST_BANKS[2 * lo // QUARTER + 1], lo, hi)
+            nc.vector.tensor_tensor(diff_first[:, lo:hi], a_sq[0][:, lo:hi], b_sq[0][:, lo:hi], ALU.subtract)
+        nc.vector.tensor_tensor(a_sq[0][:, cols(0)], diff_first[:], gain_first[:], ALU.mult)
+        scatter(0, 0, BANK)
+        squares(1, 0)
+        weigh((1, 0, BANK))
+        scatter(1, 0, BANK)
+        turn(1)
+        for t in range(HALVED):
+            make_gain(t, 1)
+            squares(t, 1)
+        weigh(*[(t, BANK, S) for t in range(HALVED)])
+        for t in range(HALVED):
+            scatter(t, BANK, S)
+        for t in range(HALVED, PACK):
+            squares(t, 0)
+            squares(t, 1)
+            make_gain(t, 1)
+            if t < PACK - 1:
+                weigh((t, 0, S))
             else:
-                square_a(t, SUM_BANKS[sums], h * BANK, (h + 1) * BANK)
-                square_b(t, SUM_BANKS[sums + 1], h * BANK, (h + 1) * BANK)
-                sums = sums + 2
-                if t < HALVED:
-                    weigh(t, cols(h))
-            if t < HALVED:
-                nc.vector.tensor_copy(page[t][:].indirect(place[:, cols(h, LIST_COLS)]), a_sq[t][:, cols(h)])
-            elif h == HALVES - 1:
-                if t == PACK - 1:
-                    weigh(t, cols(0), cols(1))
-                else:
-                    weigh(t, slice(0, S))
-                nc.vector.tensor_copy(page[t][:].indirect(place[:]), a_sq[t][:])
+                weigh((t, 0, BANK), (t, BANK, S))
+            scatter(t, 0, S)
+
+        bias_turned = bank("bias_turned", 1)
+        nc.tensor.transpose(bias_turned[:, 0:P], bias_rows[:], ident[:])
+        nc.scalar.copy(bias_col[:], bias_turned[:, 0:N_TILES])
 
         early = PACK - 1
         rounded = held("rounded", [P, early, T], BF16, tag="shared%d" % (2 * PASSES - 1))

@@ -320,19 +320,19 @@ def tile_list_tumour_board_page_kernel(
             first = c0 // 2 * PAIR
             nc.sync.dma_start(codes_out[:, c0 * BANK : c1 * BANK], page_w[c0 // 2][:, c0 * BANK - first : c1 * BANK - first])
 
-        def gate(n, c, i):
+        def gate(n, c, i, lo=0, hi=BANK):
             sig = ring.tile([P, BANK], F32, name="sig", bufs=6)
             e_sum = bank("e_sum", n % 8)
             nc.tensor.matmul_mx(
-                out=e_sum[:],
+                out=e_sum[:, lo:hi],
                 lhsT=w3_w[:, cols(i, P)].bitcast(FP8X4),
                 lhsT_scale=w3_s[:, cols(i, P)],
-                rhs=page_w[c // 2][:, cols(c % 2)].bitcast(FP8X4),
-                rhs_scale=page_s[:, cols(c)],
+                rhs=page_w[c // 2][:, c % 2 * BANK + lo : c % 2 * BANK + hi].bitcast(FP8X4),
+                rhs_scale=page_s[:, c * BANK + lo : c * BANK + hi],
                 start=True,
                 stop=True,
             )
-            nc.scalar.activation(sig[:], e_sum[:], ACT.Sigmoid, bias=bias_col[:, i : i + 1])
+            nc.scalar.activation(sig[:, lo:hi], e_sum[:, lo:hi], ACT.Sigmoid, bias=bias_col[:, i : i + 1])
             return sig
 
         def weigh_site(sig, c, i, lo, hi):
@@ -369,7 +369,6 @@ def tile_list_tumour_board_page_kernel(
         i = N_TILES - 1
         weigh_site(gate(PAIRED + 2 * i + 2, 2, i), 2, i, 0, BANK)
         store_y(i, PAIR, PAIR + BANK)
-        sig = gate(PAIRED + 2 * i + 3, 3, i)
-        for lo in (0, BANK // 2):
-            weigh_site(sig, 3, i, lo, lo + BANK // 2)
-            store_y(i, 3 * BANK + lo, 3 * BANK + lo + BANK // 2)
+        for n, (lo, hi) in enumerate(((0, 256), (256, 384), (384, 512))):
+            weigh_site(gate(PAIRED + 2 * i + 3 + n, 3, i, lo, hi), 3, i, lo, hi)
+            store_y(i, 3 * BANK + lo, 3 * BANK + hi)

@@ -60,9 +60,6 @@ def tile_list_tumour_board_page_kernel(
         def cols(index, width=BANK):
             return slice(index * width, (index + 1) * width)
 
-        def rows_of(quad, count, first=0):
-            return slice(QUAD * quad + first, QUAD * quad + first + count)
-
         pick = keep.tile([P, S // 16], U16, name="pick")
         place = keep.tile([P, S // 16], U16, name="place")
         tab_w = [held("tab_w%d" % a, [P, T], I32) for a in range(PASSES)]
@@ -114,20 +111,19 @@ def tile_list_tumour_board_page_kernel(
             nc.sync.dma_start(w2_raw[a][:], k_rows.rearrange("(p j) c -> p j c", j=PACK))
 
         def move_scale_rows(a):
-            for q in range(QUADS):
-                first = QUADS * SCALE_ROWS * a + SCALE_ROWS * q
-                nc.sync.dma_start(
-                    v_s[a][rows_of(q, SCALE_ROWS), :].bitcast(I32), v_s_rows[first : first + SCALE_ROWS, :].bitcast(I32)
-                )
+            for r in range(SCALE_ROWS):
+                first = QUADS * SCALE_ROWS * a
+                rows = v_s_rows[first + r : first + QUADS * SCALE_ROWS : SCALE_ROWS, :]
+                nc.sync.dma_start(v_s[a][r::QUAD, :].bitcast(I32), rows.bitcast(I32))
 
         nc.sync.dma_start(tab_s[0:QUAD, :].bitcast(I32), tab_scales.rearrange("a q t -> (a q) t").bitcast(I32))
         nc.sync.dma_start(pick[:], offs)
         nc.sync.dma_start(wgs_raw[0][:], wgs[:, cols(0)])
         load_tab(0)
-        for q in range(QUADS):
+        for r in range(SCALE_ROWS):
             nc.sync.dma_start(
-                w1_s_raw[rows_of(q, SCALE_ROWS), :, :].bitcast(I32),
-                w1_scales[:, cols(q, SCALE_ROWS), :].rearrange("a r c -> r a c").bitcast(I32),
+                w1_s_raw[r::QUAD, :, :].bitcast(I32),
+                w1_scales[:, r::SCALE_ROWS, :].rearrange("a q c -> q a c").bitcast(I32),
             )
         load_w2(0)
         load_w2(1)
@@ -141,10 +137,8 @@ def tile_list_tumour_board_page_kernel(
         nc.sync.dma_start(page[1][:], page_rows[1])
         nc.sync.dma_start(wgs_raw[1][:], wgs[:, cols(1)])
         nc.sync.dma_start(w3_w[:], w3_words[0].rearrange("p c i -> p (c i)").bitcast(I32))
-        for q in range(QUADS):
-            nc.sync.dma_start(
-                w3_s[rows_of(q, SCALE_ROWS), :].bitcast(I32), w3_scales[0, cols(q, SCALE_ROWS), :].bitcast(I32)
-            )
+        for r in range(SCALE_ROWS):
+            nc.sync.dma_start(w3_s[r::QUAD, :].bitcast(I32), w3_scales[0, r::SCALE_ROWS, :].bitcast(I32))
         nc.sync.dma_start(bias_rows[0:N_TILES, :], bias.rearrange("(i p) -> i p", p=P))
         site_rows = site.rearrange("(i p) m -> p i m", p=P)
         nc.sync.dma_start(site_parts[0][:], site_rows[:, :SITE_FIRST, :])
@@ -354,10 +348,8 @@ def tile_list_tumour_board_page_kernel(
         store_codes(2, 3)
         quantize_page(3)
         store_codes(3, 4)
-        for q in range(QUADS):
-            nc.sync.dma_start(
-                out_3[0, cols(q, SCALE_ROWS), :].bitcast(I32), page_s[rows_of(q, SCALE_ROWS), :].bitcast(I32)
-            )
+        for r in range(SCALE_ROWS):
+            nc.sync.dma_start(out_3[0, r::SCALE_ROWS, :].bitcast(I32), page_s[r::QUAD, :].bitcast(I32))
         for c in range(2):
             for i in range(N_TILES):
                 weigh_site(gate(N_TILES * c + i, c, i), c, i, 0, BANK)

@@ -32,10 +32,11 @@ N_TILES = N // P
 QUARTER = BANK // 2
 HALVED = 2
 SITE_FIRST = 3
-FIRST_BANKS = (5, 6, 7, 1)
-SUM_BANKS = ((None, (6, 0)), ((3, 4), (7, 1)), ((4, 6), (2, 5)), ((2, 5), (2, 5)))
+A_BANKS = ((5, 7), (6, 1), (5, 7), (2, 2))
+B_BANKS = ((None, 1), (7, 0), (6, 4), (1, 1))
+FIRST_B_BANKS = (5, 6)
 TURN_BANKS = (0, 3)
-BACK_BANKS = ((None, 3, 4, 3), (2, 5, 0, 2))
+BACK_BANKS = ((None, 3, 4, 3), (2, 1, 0, 0))
 PAGE_BF_ON = ("tab_w0", "tab_w1", "w2_raw0", "w2_raw1")
 LAST_WIDTHS = (512, 256, 256)
 PAIRED = 2 * N_TILES - 2
@@ -64,8 +65,7 @@ def tile_list_tumour_board_page_kernel(
         place = keep.tile([P, S // 16], U16, name="place")
         tab_w = [held("tab_w%d" % a, [P, T], I32) for a in range(PASSES)]
         tab_s = held("tab_s", [P, T], U8)
-        runs = (((0, BANK), (BANK, S)), ((0, QUARTER), (QUARTER, BANK), (BANK, S)))
-        v_w = [[held("v_w%d_%d" % (a, lo), [P, hi - lo], U32) for lo, hi in runs[a]] for a in range(PASSES)]
+        v_w = [[held("v_w%d_%d" % (a, h), [P, BANK], U32) for h in range(HALVES)] for a in range(PASSES)]
         v_s_rows = held("v_s_rows", [P, S], U8)
         v_s = [held("v_s%d" % a, [P, S], U8) for a in range(PASSES)]
         w1_raw = held("w1_raw", [P, PASSES, 2 * H], U8)
@@ -73,7 +73,8 @@ def tile_list_tumour_board_page_kernel(
         w1_w = [held("w1_w%d" % a, [P, 2 * H], U8, tag="shared%d" % a) for a in range(PASSES)]
         w1_s = held("w1_s", [P, PASSES, H], U8)
         w2_raw = [held("w2_raw%d" % a, [P, PACK, H], F32) for a in range(PASSES)]
-        w2_bf = [held("w2_bf%d" % a, [P, PACK * H], BF16) for a in range(PASSES)]
+        w2_bf_first = held("w2_bf0", [P, PACK * H], BF16)
+        w2_bf_last = [held("w2_bf1_%d" % u, [P, PACK * H // 2], BF16) for u in range(2)]
         w2_w = [held("w2_w%d" % a, [P, H], U32, tag="shared%d" % (PASSES + a)) for a in range(PASSES)]
         w2_s = [held("w2_s%d" % a, [P, H], U8) for a in range(PASSES)]
         wgs_raw = [held("wgs_raw%d" % h, [P, BANK], F32) for h in range(HALVES)]
@@ -125,13 +126,13 @@ def tile_list_tumour_board_page_kernel(
                 w1_s_raw[r::QUAD, :, :].bitcast(I32),
                 w1_scales[:, r::SCALE_ROWS, :].rearrange("a q c -> q a c").bitcast(I32),
             )
-        load_w2(0)
-        load_w2(1)
-        nc.vector.tensor_copy(v_s_rows[:], tab_s[:].indirect(pick[:]))
-        move_scale_rows(0)
         nc.sync.dma_start(w1_raw[:].bitcast(I32), w1_words.rearrange("a p c -> p a c").bitcast(I32))
         load_tab(1)
+        nc.vector.tensor_copy(v_s_rows[:], tab_s[:].indirect(pick[:]))
+        move_scale_rows(0)
+        load_w2(0)
         move_scale_rows(1)
+        load_w2(1)
         nc.sync.dma_start(place[:], offs2)
         nc.sync.dma_start(page[0][:], page_rows[0])
         nc.sync.dma_start(page[1][:], page_rows[1])
@@ -173,16 +174,20 @@ def tile_list_tumour_board_page_kernel(
             make_gain(t, 0)
 
         def gather_words(a):
-            for words, (lo, hi) in zip(v_w[a], runs[a]):
-                nc.vector.tensor_copy(words[:], tab_w[a][:].bitcast(U32).indirect(pick[:, lo // 16 : hi // 16]))
+            for h in range(HALVES):
+                nc.vector.tensor_copy(v_w[a][h][:], tab_w[a][:].bitcast(U32).indirect(pick[:, cols(h, LIST_COLS)]))
+
+        def round_w2(dst, a, t0, t1, m0=0, m1=P):
+            nc.vector.tensor_copy(
+                dst[:].rearrange("p (t m j) -> p m j t", t=t1 - t0, j=PACK)[:, m0:m1],
+                w2_raw[a][:].rearrange("p j (m t) -> p m j t", t=PACK)[:, m0:m1, :, t0:t1],
+            )
+
+        def quantize_w2(src, a, t0, t1):
+            columns = slice(t0 * P, t1 * P)
+            nc.vector.quantize_mx(out=w2_w[a][:, columns].bitcast(FP8X4), scales=w2_s[a][:, columns], in_=src)
 
         gather_words(0)
-        for a in range(PASSES):
-            nc.vector.tensor_copy(
-                w2_bf[a][:].rearrange("p (t m j) -> p m j t", t=PACK, j=PACK),
-                w2_raw[a][:].rearrange("p j (m t) -> p m j t", t=PACK),
-            )
-            nc.vector.quantize_mx(out=w2_w[a][:].bitcast(FP8X4), scales=w2_s[a][:], in_=w2_bf[a][:])
         for a in range(PASSES):
             nc.vector.tensor_copy(
                 w1_w[a][:].bitcast(U16).rearrange("p (t m) -> p m t", t=PACK),
@@ -192,33 +197,38 @@ def tile_list_tumour_board_page_kernel(
             w1_s[:].rearrange("p a (t m) -> p a t m", t=PACK), w1_s_raw[:].rearrange("p a (m t) -> p a t m", t=PACK)
         )
         gather_words(1)
+        round_w2(w2_bf_first, 0, 0, PACK)
+        quantize_w2(w2_bf_first[:], 0, 0, PACK)
+        round_w2(w2_bf_last[0], 1, 0, 2)
+        for t in range(2):
+            quantize_w2(w2_bf_last[0][:, cols(t, PACK * P)], 1, t, t + 1)
+        for u in range(2):
+            round_w2(w2_bf_last[1], 1, 2, PACK, u * P // 2, (u + 1) * P // 2)
+        quantize_w2(w2_bf_last[1][:], 1, 2, PACK)
 
-        def square(squares, number, lo, hi, weights, scales):
+        def square(squares, number, lo, hi, weights, scales, order):
             total = bank("total", number)
-            steps = []
-            for a in range(PASSES):
-                for words, (first, last) in zip(v_w[a], runs[a]):
-                    if first < hi and lo < last:
-                        steps.append((a, words, first, max(lo, first), min(hi, last)))
-            for n, (a, words, first, j0, j1) in enumerate(steps):
+            first = lo // BANK * BANK
+            for a in order:
                 nc.tensor.matmul_mx(
-                    out=total[:, j0 - lo : j1 - lo],
+                    out=total[:, : hi - lo],
                     lhsT=weights[a],
                     lhsT_scale=scales[a],
-                    rhs=words[:, j0 - first : j1 - first].bitcast(FP8X4),
-                    rhs_scale=v_s[a][:, j0:j1],
-                    start=(n == 0),
-                    stop=(n == len(steps) - 1),
+                    rhs=v_w[a][lo // BANK][:, lo - first : hi - first].bitcast(FP8X4),
+                    rhs_scale=v_s[a][:, lo:hi],
+                    start=(a == order[0]),
+                    stop=(a == order[-1]),
                 )
             nc.scalar.activation(squares[:, lo:hi], total[:, : hi - lo], ACT.Square)
 
-        def square_a(t, number, lo, hi):
+        def square_a(t, h):
             weights = [w1_w[a][:, cols(t, 2 * P)].bitcast(FP4X4) for a in range(PASSES)]
-            square(a_sq[t], number, lo, hi, weights, [w1_s[:, a, cols(t, P)] for a in range(PASSES)])
+            scales = [w1_s[:, a, cols(t, P)] for a in range(PASSES)]
+            square(a_sq[t], A_BANKS[t][h], h * BANK, (h + 1) * BANK, weights, scales, (0, 1))
 
-        def square_b(t, number, lo, hi):
+        def square_b(t, number, lo, hi, order):
             weights = [w2_w[a][:, cols(t, P)].bitcast(FP8X4) for a in range(PASSES)]
-            square(b_sq[t], number, lo, hi, weights, [w2_s[a][:, cols(t, P)] for a in range(PASSES)])
+            square(b_sq[t], number, lo, hi, weights, [w2_s[a][:, cols(t, P)] for a in range(PASSES)], order)
 
         def weigh(*parts):
             diff = held("diff", [P, S], F32)
@@ -231,34 +241,37 @@ def tile_list_tumour_board_page_kernel(
             for (t, lo, hi), place_of_diff in zip(parts, places):
                 nc.gpsimd.tensor_tensor(a_sq[t][:, lo:hi], place_of_diff, gain[t][:, lo:hi], ALU.mult)
 
-        def squares(t, h):
-            square_a(t, SUM_BANKS[t][h][0], h * BANK, (h + 1) * BANK)
-            square_b(t, SUM_BANKS[t][h][1], h * BANK, (h + 1) * BANK)
+        def late_b(t, h):
+            square_b(t, B_BANKS[t][h], h * BANK, (h + 1) * BANK, (1, 0))
 
         def scatter(t, lo, hi):
             nc.vector.tensor_copy(page[t][:].indirect(place[:, lo // 16 : hi // 16]), a_sq[t][:, lo:hi])
 
         diff_first = held("diff_first", [P, BANK], F32, tag="w2_bf0")
+        for h in range(HALVES):
+            for t in range(HALVED):
+                square_a(t, h)
         for lo in range(0, BANK, QUARTER):
             hi = lo + QUARTER
-            square_a(0, FIRST_BANKS[2 * lo // QUARTER], lo, hi)
-            square_b(0, FIRST_BANKS[2 * lo // QUARTER + 1], lo, hi)
+            square_b(0, FIRST_B_BANKS[lo // QUARTER], lo, hi, (0, 1))
             nc.vector.tensor_tensor(diff_first[:, lo:hi], a_sq[0][:, lo:hi], b_sq[0][:, lo:hi], ALU.subtract)
         nc.vector.tensor_tensor(a_sq[0][:, cols(0)], diff_first[:], gain_first[:], ALU.mult)
         scatter(0, 0, BANK)
-        squares(1, 0)
+        square_b(1, B_BANKS[1][0], 0, BANK, (0, 1))
         weigh((1, 0, BANK))
         scatter(1, 0, BANK)
+        for t in range(HALVED):
+            late_b(t, 1)
         turn(1)
         for t in range(HALVED):
             make_gain(t, 1)
-            squares(t, 1)
         weigh(*[(t, BANK, S) for t in range(HALVED)])
         for t in range(HALVED):
             scatter(t, BANK, S)
         for t in range(HALVED, PACK):
-            squares(t, 0)
-            squares(t, 1)
+            for h in range(HALVES):
+                square_a(t, h)
+                late_b(t, h)
             make_gain(t, 1)
             if t < PACK - 1:
                 weigh((t, 0, S))
@@ -266,7 +279,7 @@ def tile_list_tumour_board_page_kernel(
                 weigh((t, 0, BANK), (t, BANK, S))
             scatter(t, 0, S)
 
-        bias_turned = bank("bias_turned", 1)
+        bias_turned = bank("bias_turned", 4)
         nc.tensor.transpose(bias_turned[:, 0:P], bias_rows[:], ident[:])
         nc.scalar.copy(bias_col[:], bias_turned[:, 0:N_TILES])
 

@@ -37,7 +37,7 @@ B_BANKS = ((None, 1), (7, 0), (6, 4), (1, 1))
 FIRST_B_BANKS = (5, 6)
 TURN_BANKS = (0, 3)
 BACK_BANKS = ((None, 3, 4, 3), (2, 1, 0, 0))
-PAGE_BF_ON = ("tab_w0", "tab_w1", "w2_raw0", "w2_raw1")
+PAGE_BF_ON = ("tab_w0", "tab_w1")
 LAST_WIDTHS = (512, 256, 256)
 PAIRED = 2 * N_TILES - 2
 
@@ -255,7 +255,9 @@ def tile_list_tumour_board_page_kernel(
             hi = lo + QUARTER
             square_b(0, FIRST_B_BANKS[lo // QUARTER], lo, hi, (0, 1))
             nc.vector.tensor_tensor(diff_first[:, lo:hi], a_sq[0][:, lo:hi], b_sq[0][:, lo:hi], ALU.subtract)
-        nc.vector.tensor_tensor(a_sq[0][:, cols(0)], diff_first[:], gain_first[:], ALU.mult)
+        for u in range(2):
+            part = cols(u, QUARTER)
+            nc.vector.tensor_tensor(a_sq[0][:, part], diff_first[:, part], gain_first[:, part], ALU.mult)
         scatter(0, 0, BANK)
         square_b(1, B_BANKS[1][0], 0, BANK, (0, 1))
         weigh((1, 0, BANK))
@@ -285,13 +287,14 @@ def tile_list_tumour_board_page_kernel(
 
         early = PACK - 1
         rounded = held("rounded", [P, early, T], BF16, tag="shared%d" % (2 * PASSES - 1))
-        page_bf = [held("page_bf%d" % c, [P, BANK, PACK], BF16, tag=PAGE_BF_ON[c]) for c in range(CHUNKS)]
+        page_bf_pairs = [held("page_bf%d" % g, [P, 2, BANK, PACK], BF16, tag=PAGE_BF_ON[g]) for g in range(CHUNKS // 2)]
+        page_bf = [page_bf_pairs[c // 2][:, c % 2] for c in range(CHUNKS)]
 
         def pool_copy(dst, src):
             nc.gpsimd.tensor_scalar(dst, src, 1.0, 0.0, ALU.mult, ALU.add)
 
         def weave(c, count):
-            dst = page_bf[c][:].rearrange("p (g i) t -> p g t i", i=4)[:, :, 0:count, :]
+            dst = page_bf[c].rearrange("p (g i) t -> p g t i", i=4)[:, :, 0:count, :]
             nc.scalar.copy(dst, rounded[:, 0:count, cols(c)].rearrange("p t (g i) -> p g t i", i=4))
 
         for t in range(PACK):
@@ -303,13 +306,11 @@ def tile_list_tumour_board_page_kernel(
                     weave(c, t + 1)
             if t == early - 1:
                 nc.scalar.copy(rounded[:, t, PAIR:], page[t][:, PAIR:])
-                for c in range(CHUNKS):
-                    if c < CHUNKS // 2:
-                        src = page[t][:, cols(c)]
-                        pool_copy(page_bf[c][:, 2:, t], src[:, 2:])
-                        pool_copy(page_bf[c][:, 0:2, t:], src[:, 0:2].unsqueeze(2).to_broadcast([P, 2, 2]))
-                    else:
-                        weave(c, t + 1)
+                src = page[t][:, :PAIR].rearrange("p (c m) -> p c m", c=2)
+                pool_copy(page_bf_pairs[0][:, :, 2:, t], src[:, :, 2:])
+                pool_copy(page_bf_pairs[0][:, :, 0:2, t:], src[:, :, 0:2].unsqueeze(3).to_broadcast([P, 2, 2, 2]))
+                for c in range(CHUNKS // 2, CHUNKS):
+                    weave(c, t + 1)
 
         codes_out = out_2[0].rearrange("p m i -> p (m i)").bitcast(I32)
 
@@ -320,7 +321,7 @@ def tile_list_tumour_board_page_kernel(
             nc.vector.quantize_mx(
                 out=page_w[c // 2][:, cols(c % 2)].bitcast(FP8X4),
                 scales=page_s[:, cols(c)],
-                in_=page_bf[c][:].rearrange("p m t -> p (m t)"),
+                in_=page_bf[c].rearrange("p m t -> p (m t)"),
             )
 
         def store_codes(c0, c1):

@@ -302,15 +302,17 @@ def tile_list_tumour_board_page_kernel(
             if t < early - 1:
                 nc.scalar.copy(rounded[:, t, :], page[t][:])
             if t == early - 2:
-                for c in range(CHUNKS // 2):
+                for c in range(CHUNKS - 1):
                     weave(c, t + 1)
             if t == early - 1:
-                nc.scalar.copy(rounded[:, t, PAIR:], page[t][:, PAIR:])
+                nc.scalar.copy(rounded[:, t, cols(CHUNKS - 1)], page[t][:, cols(CHUNKS - 1)])
                 src = page[t][:, :PAIR].rearrange("p (c m) -> p c m", c=2)
                 pool_copy(page_bf_pairs[0][:, :, 2:, t], src[:, :, 2:])
                 pool_copy(page_bf_pairs[0][:, :, 0:2, t:], src[:, :, 0:2].unsqueeze(3).to_broadcast([P, 2, 2, 2]))
-                for c in range(CHUNKS // 2, CHUNKS):
-                    weave(c, t + 1)
+                src = page[t][:, cols(2)]
+                pool_copy(page_bf[2][:, 2:, t], src[:, 2:])
+                pool_copy(page_bf[2][:, 0:2, t:], src[:, 0:2].unsqueeze(2).to_broadcast([P, 2, 2]))
+                weave(CHUNKS - 1, t + 1)
 
         codes_out = out_2[0].rearrange("p m i -> p (m i)").bitcast(I32)
 

from contextlib import ExitStack

import concourse.mybir as mybir
from concourse.masks import make_identity

K, H, N, T, S = 1024, 512, 640, 2048, 1024
FLOPS = 2 * (2 * K * H * S + H * N * T)

F32 = mybir.dt.float32
BF16 = mybir.dt.bfloat16
I32 = mybir.dt.int32
U32 = mybir.dt.uint32
U16 = mybir.dt.uint16
U8 = mybir.dt.uint8
FP8X4 = mybir.dt.float8_e4m3fn_x4
FP4X4 = mybir.dt.float4_e2m1fn_x4
ACT = mybir.ActivationFunctionType
ALU = mybir.AluOpType

P = 128
PACK = 4
QUAD = 32
QUADS = P // QUAD
SCALE_ROWS = 4
BANK = 512
PASSES = K // (P * PACK)
HALVES = S // BANK
LIST_COLS = BANK // 16
CHUNKS = T // BANK
PAIR = 2 * BANK
N_TILES = N // P
QUARTER = BANK // 2
HALVED = 2
SITE_FIRST = 3
A_BANKS = ((5, 7), (6, 1), (5, 7), (2, 2))
B_BANKS = ((None, 1), (7, 0), (6, 4), (1, 1))
FIRST_B_BANKS = (5, 6)
TURN_BANKS = (0, 3)
BACK_BANKS = ((None, 3, 4, 3), (2, 1, 0, 0))
PAGE_BF_ON = ("tab_w0", "tab_w1")
LAST_WIDTHS = (512, 256, 256)
PAIRED = 2 * N_TILES - 2


def tile_list_tumour_board_page_kernel(
    tc, tab_words, tab_scales, offs, offs2, w1_words, w1_scales, w2, wgs, page0, w3_words, w3_scales, bias, site,
    out_0, out_1, out_2, out_3,
):
    nc = tc.nc
    with ExitStack() as ctx:
        keep = ctx.enter_context(tc.tile_pool(name="keep", bufs=1))
        ring = ctx.enter_context(tc.tile_pool(name="ring", bufs=4))
        psum = ctx.enter_context(tc.psum_pool(name="psum", bufs=1))

        def held(name, shape, dtype, tag=""):
            return keep.tile(shape, dtype, name=name, tag=tag or name, align_bytes=64)

        def bank(name, number):
            return psum.tile([P, BANK], F32, name=name, tag="bank%d" % number)

        def cols(index, width=BANK):
            return slice(index * width, (index + 1) * width)

        pick = keep.tile([P, S // 16], U16, name="pick")
        place = keep.tile([P, S // 16], U16, name="place")
        tab_w = [held("tab_w%d" % a, [P, T], I32) for a in range(PASSES)]
        tab_s = held("tab_s", [P, T], U8)
        v_w = [[held("v_w%d_%d" % (a, h), [P, BANK], U32) for h in range(HALVES)] for a in range(PASSES)]
        v_s_rows = held("v_s_rows", [P, S], U8)
        v_s = [held("v_s%d" % a, [P, S], U8) for a in range(PASSES)]
        w1_raw = held("w1_raw", [P, PASSES, 2 * H], U8)
        w1_s_raw = held("w1_s_raw", [P, PASSES, H], U8)
        w1_w = [held("w1_w%d" % a, [P, 2 * H], U8, tag="shared%d" % a) for a in range(PASSES)]
        w1_s = held("w1_s", [P, PASSES, H], U8)
        w2_raw = [held("w2_raw%d" % a, [P, PACK, H], F32) for a in range(PASSES)]
        w2_bf_first = held("w2_bf0", [P, PACK * H], BF16)
        w2_bf_last = [held("w2_bf1_%d" % u, [P, PACK * H // 2], BF16) for u in range(2)]
        w2_w = [held("w2_w%d" % a, [P, H], U32, tag="shared%d" % (PASSES + a)) for a in range(PASSES)]
        w2_s = [held("w2_s%d" % a, [P, H], U8) for a in range(PASSES)]
        wgs_raw = [held("wgs_raw%d" % h, [P, BANK], F32) for h in range(HALVES)]
        gain = [held("gain%d" % t, [P, S], F32) for t in range(PACK)]
        page = [held("page%d" % t, [P, T], F32) for t in range(PACK)]
        a_sq = [held("a_sq%d" % t, [P, S], F32) for t in range(PACK)]
        b_sq = [held("b_sq%d" % t, [P, S], F32) for t in range(PACK)]
        w3_w = held("w3_w", [P, N], I32)
        w3_s = held("w3_s", [P, N], U8)
        bias_rows = held("bias_rows", [P, P], F32)
        bias_col = held("bias_col", [P, N_TILES], F32)
        site_parts = (held("site_first", [P, SITE_FIRST, T], F32), held("site_rest", [P, N_TILES - SITE_FIRST, T], F32))
        site_t = [site_parts[i // SITE_FIRST][:, i % SITE_FIRST, :] for i in range(N_TILES)]
        page_w = [held("page_w%d" % g, [P, PAIR], I32) for g in range(CHUNKS // 2)]
        page_s = held("page_s", [P, T], U8)
        ident = held("ident", [P, P], F32)

        nc.vector.memset(tab_s[QUAD : 2 * QUAD, :].bitcast(I32), 0)
        nc.vector.memset(tab_s[2 * QUAD :, :].bitcast(I32), 0)
        for scale_tile in (w1_s_raw[:].rearrange("p a c -> p (a c)"), v_s[0][:], v_s[1][:], w3_s[:]):
            nc.vector.memset(scale_tile.bitcast(I32), 0)
        make_identity(nc, ident[:])
        nc.gpsimd.memset(bias_rows[:], 0.0)
        warm = held("warm", [P, 1], F32)
        nc.scalar.activation(warm[:], ident[:, 0:1], ACT.Sigmoid)

        page_rows = page0.rearrange("(p t) m -> t p m", t=PACK)
        out_rows = out_1.rearrange("(p t) m -> t p m", t=PACK)

        def load_tab(a):
            nc.sync.dma_start(tab_w[a][:], tab_words[a].rearrange("p t i -> p (t i)").bitcast(I32))

        def load_w2(a):
            k_rows = w2[cols(a, P * PACK), :]
            nc.sync.dma_start(w2_raw[a][:], k_rows.rearrange("(p j) c -> p j c", j=PACK))

        def move_scale_rows(a):
            for r in range(SCALE_ROWS):
                first = QUADS * SCALE_ROWS * a
                rows = v_s_rows[first + r : first + QUADS * SCALE_ROWS : SCALE_ROWS, :]
                nc.sync.dma_start(v_s[a][r::QUAD, :].bitcast(I32), rows.bitcast(I32))

        nc.sync.dma_start(tab_s[0:QUAD, :].bitcast(I32), tab_scales.rearrange("a q t -> (a q) t").bitcast(I32))
        nc.sync.dma_start(pick[:], offs)
        nc.sync.dma_start(wgs_raw[0][:], wgs[:, cols(0)])
        load_tab(0)
        for r in range(SCALE_ROWS):
            nc.sync.dma_start(
                w1_s_raw[r::QUAD, :, :].bitcast(I32),
                w1_scales[:, r::SCALE_ROWS, :].rearrange("a q c -> q a c").bitcast(I32),
            )
        nc.sync.dma_start(w1_raw[:].bitcast(I32), w1_words.rearrange("a p c -> p a c").bitcast(I32))
        load_tab(1)
        nc.vector.tensor_copy(v_s_rows[:], tab_s[:].indirect(pick[:]))
        move_scale_rows(0)
        load_w2(0)
        move_scale_rows(1)
        load_w2(1)
        nc.sync.dma_start(place[:], offs2)
        nc.sync.dma_start(page[0][:], page_rows[0])
        nc.sync.dma_start(page[1][:], page_rows[1])
        nc.sync.dma_start(wgs_raw[1][:], wgs[:, cols(1)])
        nc.sync.dma_start(w3_w[:], w3_words[0].rearrange("p c i -> p (c i)").bitcast(I32))
        for r in range(SCALE_ROWS):
            nc.sync.dma_start(w3_s[r::QUAD, :].bitcast(I32), w3_scales[0, r::SCALE_ROWS, :].bitcast(I32))
        nc.sync.dma_start(bias_rows[0:N_TILES, :], bias.rearrange("(i p) -> i p", p=P))
        site_rows = site.rearrange("(i p) m -> p i m", p=P)
        nc.sync.dma_start(site_parts[0][:], site_rows[:, :SITE_FIRST, :])
        nc.sync.dma_start(page[2][:], page_rows[2])
        nc.sync.dma_start(page[3][:], page_rows[3])
        nc.sync.dma_start(site_parts[1][:], site_rows[:, SITE_FIRST:, :])

        gain_first = bank("gain_first", 2)
        turned = []

        def turn(h):
            first = bank("turned%d" % h, TURN_BANKS[h])
            for b in range(BANK // P):
                nc.tensor.transpose(first[:, cols(b, P)], wgs_raw[h][:, cols(b, P)], ident[:])
            turned.append(first)

        def make_gain(t, h):
            spread = ring.tile([P, BANK], F32, name="spread")
            picked = turned[h][:].rearrange("p (b m t) -> p t b m", t=PACK, m=QUAD)[:, t]
            nc.scalar.copy(
                spread[:].rearrange("p (b q m) -> p b q m", q=QUADS, m=QUAD),
                picked.unsqueeze(2).to_broadcast([P, BANK // P, QUADS, QUAD]),
            )
            back = gain_first if t == h == 0 else bank("back", BACK_BANKS[h][t])
            for b in range(BANK // P):
                nc.tensor.transpose(back[:, cols(b, P)], spread[:, cols(b, P)], ident[:])
            if back is not gain_first:
                nc.scalar.copy(gain[t][:, cols(h)], back[:])

        turn(0)
        for t in range(PACK):
            make_gain(t, 0)

        def gather_words(a):
            for h in range(HALVES):
                nc.vector.tensor_copy(v_w[a][h][:], tab_w[a][:].bitcast(U32).indirect(pick[:, cols(h, LIST_COLS)]))

        def round_w2(dst, a, t0, t1, m0=0, m1=P):
            nc.vector.tensor_copy(
                dst[:].rearrange("p (t m j) -> p m j t", t=t1 - t0, j=PACK)[:, m0:m1],
                w2_raw[a][:].rearrange("p j (m t) -> p m j t", t=PACK)[:, m0:m1, :, t0:t1],
            )

        def quantize_w2(src, a, t0, t1):
            columns = slice(t0 * P, t1 * P)
            nc.vector.quantize_mx(out=w2_w[a][:, columns].bitcast(FP8X4), scales=w2_s[a][:, columns], in_=src)

        gather_words(0)
        for a in range(PASSES):
            nc.vector.tensor_copy(
                w1_w[a][:].bitcast(U16).rearrange("p (t m) -> p m t", t=PACK),
                w1_raw[:, a, :].bitcast(U16).rearrange("p (m t) -> p m t", t=PACK),
            )
        nc.gpsimd.tensor_copy(
            w1_s[:].rearrange("p a (t m) -> p a t m", t=PACK), w1_s_raw[:].rearrange("p a (m t) -> p a t m", t=PACK)
        )
        gather_words(1)
        round_w2(w2_bf_first, 0, 0, PACK)
        quantize_w2(w2_bf_first[:], 0, 0, PACK)
        round_w2(w2_bf_last[0], 1, 0, 2)
        for t in range(2):
            quantize_w2(w2_bf_last[0][:, cols(t, PACK * P)], 1, t, t + 1)
        for u in range(2):
            round_w2(w2_bf_last[1], 1, 2, PACK, u * P // 2, (u + 1) * P // 2)
        quantize_w2(w2_bf_last[1][:], 1, 2, PACK)

        def square(squares, number, lo, hi, weights, scales, order):
            total = bank("total", number)
            first = lo // BANK * BANK
            for a in order:
                nc.tensor.matmul_mx(
                    out=total[:, : hi - lo],
                    lhsT=weights[a],
                    lhsT_scale=scales[a],
                    rhs=v_w[a][lo // BANK][:, lo - first : hi - first].bitcast(FP8X4),
                    rhs_scale=v_s[a][:, lo:hi],
                    start=(a == order[0]),
                    stop=(a == order[-1]),
                )
            nc.scalar.activation(squares[:, lo:hi], total[:, : hi - lo], ACT.Square)

        def square_a(t, h):
            weights = [w1_w[a][:, cols(t, 2 * P)].bitcast(FP4X4) for a in range(PASSES)]
            scales = [w1_s[:, a, cols(t, P)] for a in range(PASSES)]
            square(a_sq[t], A_BANKS[t][h], h * BANK, (h + 1) * BANK, weights, scales, (0, 1))

        def square_b(t, number, lo, hi, order):
            weights = [w2_w[a][:, cols(t, P)].bitcast(FP8X4) for a in range(PASSES)]
            square(b_sq[t], number, lo, hi, weights, [w2_s[a][:, cols(t, P)] for a in range(PASSES)], order)

        def weigh(*parts):
            diff = held("diff", [P, S], F32)
            room = 0
            places = []
            for t, lo, hi in parts:
                places.append(diff[:, room : room + hi - lo])
                room = room + hi - lo
                nc.gpsimd.tensor_tensor(places[-1], a_sq[t][:, lo:hi], b_sq[t][:, lo:hi], ALU.subtract)
            for (t, lo, hi), place_of_diff in zip(parts, places):
                nc.gpsimd.tensor_tensor(a_sq[t][:, lo:hi], place_of_diff, gain[t][:, lo:hi], ALU.mult)

        def late_b(t, h):
            square_b(t, B_BANKS[t][h], h * BANK, (h + 1) * BANK, (1, 0))

        def scatter(t, lo, hi):
            nc.vector.tensor_copy(page[t][:].indirect(place[:, lo // 16 : hi // 16]), a_sq[t][:, lo:hi])

        diff_first = held("diff_first", [P, BANK], F32, tag="w2_bf0")
        for h in range(HALVES):
            for t in range(HALVED):
                square_a(t, h)
        for lo in range(0, BANK, QUARTER):
            hi = lo + QUARTER
            square_b(0, FIRST_B_BANKS[lo // QUARTER], lo, hi, (0, 1))
            nc.vector.tensor_tensor(diff_first[:, lo:hi], a_sq[0][:, lo:hi], b_sq[0][:, lo:hi], ALU.subtract)
        for u in range(2):
            part = cols(u, QUARTER)
            nc.vector.tensor_tensor(a_sq[0][:, part], diff_first[:, part], gain_first[:, part], ALU.mult)
        scatter(0, 0, BANK)
        square_b(1, B_BANKS[1][0], 0, BANK, (0, 1))
        weigh((1, 0, BANK))
        scatter(1, 0, BANK)
        for t in range(HALVED):
            late_b(t, 1)
        turn(1)
        for t in range(HALVED):
            make_gain(t, 1)
        weigh(*[(t, BANK, S) for t in range(HALVED)])
        for t in range(HALVED):
            scatter(t, BANK, S)
        for t in range(HALVED, PACK):
            for h in range(HALVES):
                square_a(t, h)
                late_b(t, h)
            make_gain(t, 1)
            if t < PACK - 1:
                weigh((t, 0, S))
            else:
                weigh((t, 0, BANK), (t, BANK, S))
            scatter(t, 0, S)

        bias_turned = bank("bias_turned", 4)
        nc.tensor.transpose(bias_turned[:, 0:P], bias_rows[:], ident[:])
        nc.scalar.copy(bias_col[:], bias_turned[:, 0:N_TILES])

        early = PACK - 1
        rounded = held("rounded", [P, early, T], BF16, tag="shared%d" % (2 * PASSES - 1))
        page_bf_pairs = [held("page_bf%d" % g, [P, 2, BANK, PACK], BF16, tag=PAGE_BF_ON[g]) for g in range(CHUNKS // 2)]
        page_bf = [page_bf_pairs[c // 2][:, c % 2] for c in range(CHUNKS)]

        def pool_copy(dst, src):
            nc.gpsimd.tensor_scalar(dst, src, 1.0, 0.0, ALU.mult, ALU.add)

        def weave(c, count):
            dst = page_bf[c].rearrange("p (g i) t -> p g t i", i=4)[:, :, 0:count, :]
            nc.scalar.copy(dst, rounded[:, 0:count, cols(c)].rearrange("p t (g i) -> p g t i", i=4))

        for t in range(PACK):
            nc.sync.dma_start(out_rows[t], page[t][:])
            if t < early - 1:
                nc.scalar.copy(rounded[:, t, :], page[t][:])
            if t == early - 2:
                for c in range(CHUNKS - 1):
                    weave(c, t + 1)
            if t == early - 1:
                nc.scalar.copy(rounded[:, t, cols(CHUNKS - 1)], page[t][:, cols(CHUNKS - 1)])
                src = page[t][:, :PAIR].rearrange("p (c m) -> p c m", c=2)
                pool_copy(page_bf_pairs[0][:, :, 2:, t], src[:, :, 2:])
                pool_copy(page_bf_pairs[0][:, :, 0:2, t:], src[:, :, 0:2].unsqueeze(3).to_broadcast([P, 2, 2, 2]))
                src = page[t][:, cols(2)]
                pool_copy(page_bf[2][:, 2:, t], src[:, 2:])
                pool_copy(page_bf[2][:, 0:2, t:], src[:, 0:2].unsqueeze(2).to_broadcast([P, 2, 2]))
                weave(CHUNKS - 1, t + 1)

        codes_out = out_2[0].rearrange("p m i -> p (m i)").bitcast(I32)

        def round_last_slice(copy, c):
            copy(page_bf[c][:, :, PACK - 1], page[PACK - 1][:, cols(c)])

        def quantize_page(c):
            nc.vector.quantize_mx(
                out=page_w[c // 2][:, cols(c % 2)].bitcast(FP8X4),
                scales=page_s[:, cols(c)],
                in_=page_bf[c].rearrange("p m t -> p (m t)"),
            )

        def store_codes(c0, c1):
            first = c0 // 2 * PAIR
            nc.sync.dma_start(codes_out[:, c0 * BANK : c1 * BANK], page_w[c0 // 2][:, c0 * BANK - first : c1 * BANK - first])

        def gate(n, c, i, lo=0, hi=BANK):
            sig = ring.tile([P, BANK], F32, name="sig", bufs=6)
            e_sum = bank("e_sum", n % 8)
            nc.tensor.matmul_mx(
                out=e_sum[:, lo:hi],
                lhsT=w3_w[:, cols(i, P)].bitcast(FP8X4),
                lhsT_scale=w3_s[:, cols(i, P)],
                rhs=page_w[c // 2][:, c % 2 * BANK + lo : c % 2 * BANK + hi].bitcast(FP8X4),
                rhs_scale=page_s[:, c * BANK + lo : c * BANK + hi],
                start=True,
                stop=True,
            )
            nc.scalar.activation(sig[:, lo:hi], e_sum[:, lo:hi], ACT.Sigmoid, bias=bias_col[:, i : i + 1])
            return sig

        def weigh_site(sig, c, i, lo, hi):
            y = site_t[i][:, BANK * c + lo : BANK * c + hi]
            nc.vector.tensor_tensor(y, sig[:, lo:hi], y, ALU.mult)

        def store_y(i, lo, hi):
            nc.sync.dma_start(out_0[cols(i, P), lo:hi], site_t[i][:, lo:hi])

        round_last_slice(nc.vector.tensor_copy, 0)
        quantize_page(0)
        store_codes(0, 1)
        round_last_slice(nc.vector.tensor_copy, 1)
        quantize_page(1)
        store_codes(1, 2)
        round_last_slice(nc.scalar.copy, 2)
        round_last_slice(nc.scalar.copy, 3)
        quantize_page(2)
        store_codes(2, 3)
        quantize_page(3)
        store_codes(3, 4)
        for r in range(SCALE_ROWS):
            nc.sync.dma_start(out_3[0, r::SCALE_ROWS, :].bitcast(I32), page_s[r::QUAD, :].bitcast(I32))
        for c in range(2):
            for i in range(N_TILES):
                weigh_site(gate(N_TILES * c + i, c, i), c, i, 0, BANK)
                store_y(i, BANK * c, BANK * (c + 1))
        for i in range(N_TILES - 1):
            for c in range(2, CHUNKS):
                weigh_site(gate(PAIRED + 2 * i + c, c, i), c, i, 0, BANK)
                store_y(i, BANK * c, BANK * (c + 1))
        i = N_TILES - 1
        weigh_site(gate(PAIRED + 2 * i + 2, 2, i), 2, i, 0, BANK)
        store_y(i, PAIR, PAIR + BANK)
        for n, (lo, hi) in enumerate(((0, 256), (256, 384), (384, 512))):
            weigh_site(gate(PAIRED + 2 * i + 3 + n, 3, i, lo, hi), 3, i, lo, hi)
            store_y(i, 3 * BANK + lo, 3 * BANK + hi)
